import numpy as np, ml_dtypes
CORES = [16,17,18,19,32,33,34,35]
N = 8
import mx_ref
BF = ml_dtypes.bfloat16
def gentries(a):
    return np.ascontiguousarray(a.reshape(8, 16, -1).transpose(0, 2, 1)).reshape(8, -1)
def gtable(e):
    e = np.asarray(e); return np.ascontiguousarray(e.reshape(8, -1, 16).transpose(0, 2, 1)).reshape(128, -1).astype(np.int32)
def gcols(t, e):
    v = np.concatenate([t.reshape(8, 16, -1, 4), np.zeros((8, 16, 1, 4), BF)], axis=2)
    return np.ascontiguousarray(np.stack([v[g][:, e[g]] for g in range(8)])).reshape(128, -1)
def tile(rs):
    return np.stack(rs, axis=2).reshape(128, -1).astype(BF)
def pick(q, e):
    c = np.concatenate([q[0].reshape(128, -1, 4), np.zeros((128, 1, 4), np.uint8)], axis=1); s = np.concatenate([q[1], np.ones((16, 1), np.uint8)], axis=1)
    return (np.ascontiguousarray(c[:, e].reshape(128, -1)), np.ascontiguousarray(s[:, e]))
def join(*qs):
    return (np.concatenate([q[0] for q in qs], axis=1), np.concatenate([q[1] for q in qs], axis=1))
def put(q, e, v):
    c, s = q[0].reshape(128, -1, 4).copy(), q[1].copy(); c[:, e] = v[0].reshape(128, -1, 4); s[:, e] = v[1]
    return (c.reshape(128, -1), s)
def pk(c, s):
    return (np.ascontiguousarray(c), mx_ref.live(s))
def emit(q):
    return q[0], q[1]
def packed(v, rng):
    q = [mx_ref.quantize(np.ascontiguousarray(v[r])) for r in range(N)]
    return np.stack([a for a, b in q]), np.stack([mx_ref.plane(b, rng) for a, b in q])
def values_of_codes():
    e, c = np.zeros((128, 128, 4), np.float32), np.zeros((128, 2, 4), np.uint8)
    e[np.arange(128), np.arange(128), 0] = 1
    c[:127, :, 0] = np.arange(256).reshape(2, 128).T[:127]
    return mx_ref.matmul(mx_ref.quantize(e.reshape(128, 512).astype(BF)), (c.reshape(128, 8), np.full((16, 2), 127, np.uint8))).T.reshape(-1).astype(np.float64)
CODE_VALUE, SCALE_VALUE = values_of_codes(), 2.0 ** (np.arange(256) - 127.0)
def decode(q):
    return (CODE_VALUE[q[0]].reshape(16, 8, -1, 4) * SCALE_VALUE[q[1]][:, None, :, None] + 0.0).reshape(128, -1).astype(np.float32)
def f(rng, *shape):
    return mx_ref.flush((rng.standard_normal(shape, dtype=np.float32) * np.exp2(rng.integers(-2, 3, shape[:-1] + (1,)))).astype(BF))
def wide(rng, *shape, cols=0):
    v = rng.standard_normal(shape, dtype=np.float32) * np.exp2(rng.integers(-12, 13, shape)).astype(np.float32)
    if cols: v *= np.repeat(np.exp2(rng.integers(-cols, cols + 1, shape[:-2] + (1, shape[-1] // 4))) * (rng.random(shape[:-2] + (1, shape[-1] // 4)) > 0.0625), 4, axis=-1).astype(np.float32)
    return mx_ref.flush(v.astype(BF))
C, H, E, R = 256, 128, 384, 3
def big(v):
    v = v.astype(np.float32)
    v[np.abs(v) < np.float32(2.0 ** -16)] = 0
    return v.astype(BF)
def numbers_of(rng):
    return {"x": big(f(rng, N, 128, 4 * C)), "u": np.array(f(rng, N, 128, 512)), "v": np.array(f(rng, N, 128, 512))}
def stored(a):
    return np.stack([gtable(a[r]) for r in range(N)])
def lists(rng):
    return {"lf": stored(rng.integers(0, E, (N, 8, E))), "rt": stored(rng.integers(0, E, (N, 8, E)))}
def layers(rng, still=[]):
    w = big(f(rng, N, 128, 2048)).reshape(N, 8, 16, 4, 8, 16, 4)
    for i in still:
        w[:, :, i] = 0
        w[:, :, :, :, :, i] = 0
    return w
def weights(rng, w):
    c, p = packed(np.ascontiguousarray(w).reshape(N, 128, 2048), rng)
    return {"wc": c, "ws": p}
def setup_inputs(rng):
    return {**numbers_of(rng), **lists(rng), **weights(rng, layers(rng))}
def setup_inputs_ties(rng):
    d = numbers_of(rng)
    o = rng.permutation(N)
    x = d["x"].reshape(N, 8, 16, C, 4)
    x[:, :, 0] = 0
    x[:, :, 0, :, 0] = rng.integers(-2, 3, (N, 8, C)).astype(np.float32).astype(BF)
    u = d["u"].reshape(N, 128, 128, 4)
    u[:, :, ::16] = 0
    for h in range(0, 128, 16): u[:, h, h, 0] = 1
    u[o[0], :, ::16] = 0
    e = lists(rng)
    e["rt"][o[1]] = e["lf"][o[1]]
    return {"x": x.reshape(N, 128, 4 * C), "u": u.reshape(N, 128, 512), "v": d["v"], **e, **weights(rng, layers(rng, [0]))}
def setup_inputs_near(rng):
    d = numbers_of(rng)
    kind = rng.permutation(8) % 4
    x = d["x"].astype(np.float32).reshape(N, 8, 16, C, 4)
    c = rng.integers(0, 2, (N, 8, C)) * 2.0 - 1.0
    s = rng.integers(0, 16, (N, 8, C))
    x[:, :, 0] = 0
    x[:, :, 8:] = 0
    x[:, :, 0, :, 0] = c
    x[:, :, 8] = c[:, :, :, None] * ((s[:, :, :, None] >> np.arange(4)) & 1) * np.exp2(np.arange(4) - 23.0)
    x[:, :, 11, :, 0] = c * 2.0 ** -10
    u = d["u"].reshape(N, 128, 128, 4)
    u[:, :, ::16] = 0
    for g in range(8):
        h, m = 16 * g, 1.0 if kind[g] == 0 else 2.0 ** -30
        if kind[g] < 2:
            u[:, h, h, 0] = m
            u[:, h + 11, h, 0] = m
        if kind[g] < 3: u[:, h + 8, h] = m
        else:
            a = rng.integers(0, 2, (N, C))
            x[:, g, 8:] = 0
            x[:, g, 10, :, 0] = c[:, g] * a * 1.125 * 2.0 ** -30
            x[:, g, 10, :, 1] = c[:, g] * (1 - a) * 1.25 * 2.0 ** -30
            u[:, h + 10, h, 0] = m * 1.125
            u[:, h + 10, h, 1] = m
    x = (x + np.float32(0.0)).reshape(N, 128, 4 * C).astype(BF)
    return {"x": x, "u": u.reshape(N, 128, 512), "v": d["v"], **lists(rng), **weights(rng, layers(rng, [0, 8, 9, 10, 11, 12, 13, 14, 15]))}
def setup_inputs_twice(rng):
    d = numbers_of(rng)
    x = (2 * rng.integers(0, 8, (N, 8, 16, C, 4)) + 1) * np.exp2(rng.integers(-17, -15, (N, 8, 16, C, 4))) * (rng.integers(0, 2, (N, 8, 16, C, 4)) * 2.0 - 1.0)
    x[:, :, ::8, :, 0] = np.where(rng.random((N, 8, 2, C)) < 0.5, 1.96875, 1.75) * (rng.integers(0, 2, (N, 8, 2, C)) * 2.0 - 1.0)
    a = int(rng.integers(1, 8))
    x[:, a, ::8, :, 0] = 1.75
    t = np.arange(C) % 4 == rng.integers(0, 4, (N, 1))
    x[:, 0] = np.where(t[:, None, :, None], 0.0, x[:, 0])
    x[:, 0, ::8, :, 0] = np.where(t[:, None], 1.75 * 2.0 ** -24 * (rng.integers(0, 2, (N, 2, C)) * 2.0 - 1.0), x[:, 0, ::8, :, 0])
    u = d["u"].reshape(N, 128, 128, 4)
    u[:, ::8, ::16] = 0
    w = np.zeros((N, 128, 4, 128, 4), np.float32)
    i = np.arange(128)
    for b in range(4): w[:, i, b, i, b] = -32
    w[:, i[::16], 0, i[::16], 0] = -36
    w[:, i[8::16], 0, i[8::16], 0] = -18
    w[:, :, :, :16] = 0
    w[:, :, :, 16 * a:16 * a + 16] = 0
    m = np.arange(16)
    k = np.where(np.arange(N) % 2 == rng.integers(0, 2), 1.0, -1.0)[:, None]
    for b in range(4): w[:, 16 * a + m, b, m, b] = 32 * k
    w[:, 16 * a + m[::8], 0, m[::8], 0] = 36 * k
    e = rng.integers(0, E, (2, N, 8, E))
    for r in range(N):
        e[:, r, 0, :C] = rng.permutation(np.concatenate([np.arange(H), np.arange(C, E), H + rng.permutation(C - H)[:C - 2 * H]]))
    return {"x": x.astype(np.float32).reshape(N, 128, 4 * C).astype(BF), "u": u.reshape(N, 128, 512), "v": d["v"], "lf": stored(e[0]), "rt": stored(e[1]), **weights(rng, w.astype(BF))}
def setup_inputs_ends(rng):
    d = numbers_of(rng)
    e = rng.permutation(N)
    h = rng.permutation(8)
    most = 1.34375 * 2.0 ** 28
    x = (0.6 + 0.4 * rng.random((N, 8, 16, C, 4))) * most
    x[e[::2]] = most
    c = rng.integers(0, 2, (N, 1, 1, C, 1)) * 2.0 - 1.0
    c[e[1]] = c[e[1], 0, 0, 0, 0]
    x = x * c
    x[:, h[4:], 8:] = (rng.integers(0, 2, (N, 4, 8, C, 4)) * 2.0 - 1.0) * 2.0 ** -30
    u = d["u"].reshape(N, 128, 128, 4)
    u[:, :, ::16] = 0
    for g in h[:4]: u[:, :, 16 * g] = (2.0 ** 30 * (1.0 - 0.1 * rng.random((N, 128, 4))) * rng.choice([-1.0, 1.0], (N, 1, 1))).astype(np.float32).astype(BF)
    for g in h[4:]: u[:, 16 * g + 8:16 * g + 16, 16 * g] = 2.0 ** -30
    u[e[2], :, ::16] = 0
    v = d["v"]
    v[e[:2]] = (2.0 ** 30 * rng.choice([-1.0, 1.0], (2, 128, 512))).astype(np.float32).astype(BF)
    a = rng.integers(0, 2, (2, N, 8, E)) * (E - 1)
    a[:, e[0]] = E - 1
    a[:, e[1]] = 0
    a[:, e[2]] = np.argsort(rng.random((2, 8, E)), axis=2)
    p, m = np.arange(C), rng.permutation(C)
    for g, k in enumerate(rng.permutation(8)):
        t = rng.permutation(E)
        if k == 0: t = np.concatenate([rng.permutation(C), C + rng.permutation(H)])
        elif H * (k - 1) < C: t = np.concatenate([C + rng.permutation(H), rng.permutation(C)])
        a[0, e[2], g, np.concatenate([p[np.roll(m, -H * (k - 1))], np.setdiff1d(np.arange(E), p)])] = t
        p = a[0, e[2], g, p]
    a[:, e[3]] = rng.integers(0, C, (2, 8, E))
    w = np.zeros((N, 128, 4, 128, 4), np.float32)
    i = np.flatnonzero(np.arange(128) % 16 < 8)
    k = rng.choice([-4.0, 4.0], (N, 1))
    for b in range(4): w[:, i, b, i, b] = k
    v = (np.where(v < 0, -1.0, 1.0) * np.where(rng.permutation(N) % 2, 2.0 ** -30, 2.0 ** 30)[:, None, None]).astype(np.float32).astype(BF)
    return {"x": x.astype(np.float32).reshape(N, 128, 4 * C).astype(BF), "u": u.reshape(N, 128, 512), "v": v, "lf": stored(a[0]), "rt": stored(a[1]), **weights(rng, w.astype(BF))}
def setup_inputs_spread(rng):
    d = numbers_of(rng)
    w = (layers(rng).astype(np.float32) * np.float32(0.125)).astype(BF)
    return {"x": big(wide(rng, N, 128, 4 * C, cols=4)), "u": d["u"], "v": d["v"], **lists(rng), **weights(rng, w)}
def check_inputs(d):
    b = []
    for k in ("x", "u", "v"):
        a = np.abs(d[k].astype(np.float32))
        if not (np.isfinite(a).all() and ((a == 0) | (a >= 2.0 ** -30) & (a <= 2.0 ** 30)).all()): b.append("a value of " + k)
    for k in ("lf", "rt"):
        if not ((d[k] >= 0) & (d[k] < E)).all(): b.append("an entry of " + k)
    none, least, most = [emit(mx_ref.quantize(np.full((128, 16), k, np.float32).astype(BF)))[1][0, 0] for k in (0.0, 2.0 ** -30, 2.0 ** 30)]
    size = 0.0
    for r in range(N):
        if ((d["wc"][r] == 0x7F) | (d["wc"][r] == 0xFF)).any(): b.append("wc: a code that is no number")
        s = mx_ref.live(d["ws"][r])
        if ((s != none) & ((s < least) | (s > most))).any(): b.append("ws: a scale out of range")
        full = ((d["wc"][r] & 0x7F) != 0).reshape(16, 8, 512, 4).any(axis=(1, 3))
        if (full & (s == none)).any(): b.append("wc: a code other than zero at the scale of zeros")
        with np.errstate(all="ignore"):
            size = np.maximum(size, np.max(np.sum(np.abs(decode(pk(d["wc"][r], d["ws"][r])).astype(np.float64)).reshape(128, 512, 4), axis=(0, 2))))
    with np.errstate(all="ignore"):
        if not np.max(np.abs(d["x"].astype(np.float64))) * (1.125 + 2.5 * size * 2.0 ** -5) ** 3 <= 2.0 ** 30: b.append("the sizes of x and W together")
    return b
def reference(x, u, v, lf, rt, wc, ws):
    qu = [mx_ref.quantize(u[r]) for r in range(N)]
    lay = [pk(wc[r], ws[r]) for r in range(N)]
    left = [gentries(lf[r]) for r in range(N)]
    right = [gentries(rt[r]) for r in range(N)]
    now = [x[r] for r in range(N)]
    took = np.zeros((N, 8, C), np.int64)
    for t in range(R):
        q = [mx_ref.quantize(now[r]) for r in range(N)]
        edge = [pick(q[r], np.arange(H)) for r in range(N)]
        own = [decode(q[r]) for r in range(N)]
        flux, back = [], []
        for r in range(N):
            e = (r + 1) % N
            s = np.abs(mx_ref.matmul(qu[r], join(q[r], edge[e]))[::16])
            l, k = np.arange(C), np.arange(C)
            for g in range(8):
                a, b = left[r][g, l], right[r][g, k]
                first = s[g, a] <= s[g, b]
                took[r, g] = np.where(first, a, b)
                l, k = np.where(first, a, l), np.where(first, k, b)
            window = np.concatenate([own[r], own[e][:, :4 * H]], axis=1).astype(BF)
            z = mx_ref.quantize(gcols(window, took[r]))
            h = mx_ref.quantize(tile([mx_ref.matmul(pick(lay[r], np.arange(128 * b, 128 * b + 128)), z) * np.float32(0.03125) for b in range(4)]))
            c = np.full((8, E), -1)
            for g in range(8):
                i, j = np.unique(took[r, g], return_index=True)
                c[g, i] = j
            w = gcols(decode(h).astype(BF), c)
            flux.append(w[:, :4 * C].astype(np.float32))
            back.append(decode(mx_ref.quantize(np.ascontiguousarray(w[:, 4 * C:]))))
        for r in range(N):
            n = own[r] - flux[r]
            n[:, :4 * H] = n[:, :4 * H] - back[(r - 1) % N]
            now[r] = n.astype(BF)
    y, on = np.zeros((N, 128, C), np.float32), np.zeros((N, 8, C), np.float32)
    oc, osc = np.zeros((N, 128, 4 * C), np.uint8), np.zeros((N, 16, C), np.uint8)
    for r in range(N):
        q = mx_ref.quantize(now[r])
        y[r] = mx_ref.matmul(mx_ref.quantize(v[r]), q)
        on[r] = took[r]
        oc[r], osc[r] = emit(q)
    return {"y": y, "on": on, "oc": oc, "osc": osc}

@@ -1,0 +1,346 @@
+from concourse.mybir import dt, AluOpType, ActivationFunctionType
+
+OP = AluOpType
+AF = ActivationFunctionType
+N, R, C, H, E = 8, 3, 256, 128, 384
+CW = 800
+PW = 272
+EARLY = 4
+PRE = 4
+LISTS = ("float8_e4m3fn_x4 QX 384 QU 128 UQ 1024 QV 128 WQ 512 QE 512 QM 256 QT 256 QB 128 LB 128",
+         "uint8 SX 384 SU 128 US 1024 SV 128 WS 512 SE 512 SM 256 SQ 256 SB 128 LS 128",
+         "bfloat16 X 1024 UIN 512 VIN 512 ONES 128 IDN 128 EB 2048 VP 1536 M 1024 TT 1024 DW 1088 CELL0 800 CELL1 800 "
+         "CELL2 800 POS 256 CT 768 UB 512",
+         "float32 IOTA 768 TAB 6144 SCP 3456 STB 36 SCN 512 CS 512 GT 64 GB 32 GA 32 ZB 32 CZ 4 PB 32 PR 16 NB 16 UNW 256 "
+         "CEA 16 EE 256 DS 256 FLB 16 MXB 16 CM 24 FU 512 MASK 64 MINM 32 RM 64 CDG 256 PF 8 YO 256 ONR 256",
+         "int32 LST 384 NI 16 T1 16 MD 256 MDA 256 MI 64 PI 8 UOI 64 RPI 16 RVI 16",
+         "uint16 LSU 384 OFG 32 OFW 32 NU 16 OFN 16 OFS 32 OFC 24 UOF 64 REP 16 REV 16")
+WIDTH = {}
+SCRATCH = {}
+for _line in LISTS:
+    _w = _line.split()
+    for _i in range(1, len(_w), 2):
+        WIDTH[_w[_i]] = int(_w[_i + 1])
+        SCRATCH[_w[_i]] = ("sbuf", [128, int(_w[_i + 1])], _w[0])
+for _i in range(8):
+    WIDTH["ps%d" % _i] = 512
+    SCRATCH["ps%d" % _i] = ("psum", [128, 512], "float32")
+SEMAPHORES = ["v", "s", "pe", "gp", "lx0", "lx1", "lu", "lv", "lwc", "lws", "la", "lb", "lr", "exa", "exb", "outs", "oute",
+              "brd", "bar", "sbrd", "sbar"]
+
+
+def rank_program(g, core, T, topo):
+    rank = T.rank_of(core)
+    if rank is None:
+        return
+    nxt, prv = T.cores[(rank + 1) % N], T.cores[(rank - 1) % N]
+    v, s = g.vector, g.scalar
+    eng = {"pe": g.tensor, "v": v, "s": s, "g": g, "y": g.sync}
+    home = {"pe": "pe", "v": "v", "s": "s", "g": "gp"}
+    count = {k: 0 for k in SEMAPHORES}
+    held = {}
+    log = {}
+
+    def B(n, a=0, b=None, st=1, ix=None, bit=None, p=(0, 128)):
+        b = WIDTH[n] if b is None else b
+        ap = T[n][p[0]:p[1], a:b] if st == 1 else T[n][p[0]:p[1], a:b:st]
+        if bit:
+            ap = ap.bitcast(bit)
+        if ix:
+            ap = ap.indirect(ix[0])
+        return (ap, [(n, p[0], p[1], a, b, st)], ix[1] if ix else [])
+
+    def wait(q, sem, val):
+        if held.get((q, sem), 0) < val:
+            held[(q, sem)] = val
+            eng[q].wait_ge(T.sem[sem], val)
+
+    def order(q, reads, writes):
+        need = {}
+        for kinds, regs in (("w", reads), ("rw", writes)):
+            for n, p0, p1, c0, c1, st in regs:
+                for k, a0, a1, b0, b1, su, sem, val, far in log.get(n, ()):
+                    if k in kinds and a0 < p1 and p0 < a1 and b0 < c1 and c0 < b1 and (st != su or (c0 - b0) % st == 0):
+                        need[sem] = max(need.get(sem, 0), count[sem] if far else val)
+        for sem in need:
+            wait(q, sem, need[sem])
+
+    def note(reads, writes, sem, far):
+        for n, p0, p1, c0, c1, st in writes:
+            log[n] = [x for x in log.get(n, ()) if not (p0 <= x[1] and x[2] <= p1 and c0 <= x[3] and x[4] <= c1
+                                                        and (st == 1 or st == x[5] and (c0 - x[3]) % st == 0))]
+        for kind, regs in (("w", writes), ("r", reads)):
+            for r in regs:
+                log.setdefault(r[0], []).append((kind,) + r[1:] + (sem, count[sem], far))
+
+    def run(q, call, *args, outs=1, **kw):
+        reads, writes, real = [], [], []
+        for i, x in enumerate(args):
+            if isinstance(x, tuple):
+                (writes if i < outs else reads).extend(x[1])
+                reads.extend(x[2])
+                x = x[0]
+            real.append(x)
+        order(q, reads, writes)
+        call(*real, **kw).then_inc(T.sem[home[q]], 1)
+        count[home[q]] += 1
+        note(reads, writes, home[q], False)
+
+    def dma(q, sem, out, in_):
+        w, r = (out[1] if isinstance(out, tuple) else []), (in_[1] if isinstance(in_, tuple) else [])
+        order(q, r, w)
+        eng[q].dma_start(out[0] if isinstance(out, tuple) else out, in_[0] if isinstance(in_, tuple) else in_).then_inc(T.sem[sem], 16)
+        count[sem] += 16
+        note(r, w, sem, True)
+
+    def engines(a, b):
+        return topo.engines(a, b)[:8]
+
+    def exchange(dst, src, pairs, remote, local):
+        reads = [r for o, i in pairs for r in i[1]]
+        order("g", reads, [])
+        rid, pid, _ = topo.addr(dst)
+        es = engines(core, dst)
+        for o, i in pairs:
+            g.remote_dma(out_ap=o[0], in_ap=i[0], remote_sem=T.sem[remote], local_sem=T.sem[local], pid=pid, routing_id=rid,
+                         dma_engine_mask=sum(1 << e for e in es))
+            count[local] += len(es)
+        note(reads, [], local, True)
+        count[remote] += len(pairs) * len(engines(src, core))
+        note([], [r for o, i in pairs for r in o[1]], remote, True)
+
+    def ts(out, in0, s1, op0, s2=None, op1=None):
+        run("v", v.tensor_scalar, out, in0, s1, s2, op0, *((op1,) if op1 else ()))
+
+    def tt(out, in0, in1, op):
+        run("v", v.tensor_tensor, out, in0, in1, op)
+
+    def cp(out, in_):
+        run("v", v.tensor_copy, out, in_)
+
+    def act(out, in_, func=AF.Copy, **kw):
+        run("s", s.activation, out, in_, func, **kw)
+
+    def scan(out, d0, d1, op0, op1):
+        run("v", v.tensor_tensor_scan, out, d0, d1, 0.0, op0, op1)
+
+    def fill(x, c):
+        run("v", v.memset, x, c)
+
+    def quant(q, sc, a, b, tile):
+        run("v", v.quantize_mx, B(q, a, b), B(sc, a, b), B(tile, 4 * a, 4 * b), outs=2)
+
+    bank = [0]
+
+    def mm(lq, ls, la, rq, rs, a, b):
+        p = "ps%d" % (bank[0] % 8)
+        bank[0] += 1
+        run("pe", g.tensor.matmul_mx, B(p, 0, b - a), B(lq, la, la + 128), B(ls, la, la + 128), B(rq, a, b), B(rs, a, b), True, True)
+        return B(p, 0, b - a)
+
+    def score(k, a, b):
+        o = E * (k + 1)
+        act(B("SCP", o + a, o + b), mm("UQ", "US", 128 * k, "QX", "SX", a, b), AF.Abs)
+
+    def send_border():
+        exchange(prv, nxt, ((B("QX", C, E, bit=dt.uint8), B("QX", 0, H, bit=dt.uint8)), (B("SX", C, E), B("SX", 0, H))), "brd", "sbrd")
+
+    def iota(out, pattern, base, cm):
+        run("g", g.iota, out, pattern, base, cm, allow_small_or_imprecise_dtypes=True)
+
+    dma("y", "lx0", B("X", 0, 512), T.x[:, 0:512])
+    dma("s", "lx1", B("X", 512, 1024), T.x[:, 512:1024])
+    dma("y", "lu", B("UIN"), T.u[:])
+    for k in range(8):
+        dma("y", "la", B("LST", 48 * k, 48 * k + 24, p=(0, 16)), T.lf[16 * k:16 * k + 16, :])
+        dma("s", "lb", B("LST", 48 * k + 24, 48 * k + 48, p=(0, 16)), T.rt[16 * k:16 * k + 16, :])
+    fill(B("ONES"), 1.0)
+    fill(B("EB"), 0.0)
+    run("g", g.affine_select, B("IDN"), B("ONES"), [[-1, 128]], OP.is_equal, 0.0, 0, 1)
+    iota(B("UOI"), [[16, 8], [0, 8]], 0, 0)
+    iota(B("MD"), [[1, 256]], 256, -1)
+    iota(B("PI", 0, 1), [[1, 1]], 0, 1)
+    iota(B("MI"), [[1, 64]], 0, 0)
+    quant("QX", "SX", 0, H, "X")
+    send_border()
+    dma("s", "lwc", B("WQ", bit=dt.uint8), T.wc[:])
+    dma("s", "lws", B("WS"), T.ws[:])
+    for h in range(1, 8):
+        dma("y", "lr", B("LST", p=(16 * h, 16 * h + 16)), B("LST", p=(0, 16)))
+    dma("y", "lv", B("VIN"), T.v[:])
+    iota(B("IOTA"), [[1, 768]], 0, 0)
+    iota(B("POS"), [[1, 256]], 1, 0)
+    iota(B("RPI"), [[1, 16]], 0, 0)
+    iota(B("RVI"), [[-16, 16]], 255, 0)
+    quant("QX", "SX", H, C, "X")
+    cp(B("UOF"), B("UOI"))
+    quant("QU", "SU", 0, 128, "UIN")
+    cp(B("UQ", bit=dt.uint32), B("QU", bit=dt.uint32, ix=B("UOF")))
+    act(B("US"), B("SU", ix=B("UOF")))
+    for k in range(8):
+        score(k, 0, C)
+    ts(B("MDA"), B("MD"), 15, OP.bitwise_and)
+    ts(B("MASK"), B("MDA", 0, 64), 0, OP.is_equal)
+    ts(B("MINM"), B("MASK", 0, 32), 1e29, OP.mult, -1.0, OP.add)
+    ts(B("CDG"), B("MDA"), 0, OP.not_equal)
+    ts(B("MI"), B("MI"), 15, OP.bitwise_and)
+    ts(B("RM"), B("MI"), 0, OP.not_equal)
+    ts(B("PI", 1, 2), B("PI", 0, 1), 7, OP.bitwise_and)
+    ts(B("PI", 2, 3), B("PI", 0, 1), 3, OP.arith_shift_right)
+    ts(B("PI", 3, 4), B("PI", 0, 1), 15, OP.bitwise_and)
+    ts(B("PI", 4, 5), B("PI", 0, 1), 16, OP.bitwise_and)
+    ts(B("PF", 0, 1), B("PI", 1, 2), 32, OP.mult)
+    tt(B("PF", 1, 2), B("PF", 0, 1), B("PI", 2, 3), OP.add)
+    for x in range(4):
+        ts(B("STB", x, x + 1), B("PF", 1, 2), -1.0, OP.mult, float(255 - 16 * (x % 2) + E * (x // 2)), OP.add)
+    cp(B("OFG", 0, 4), B("STB", 0, 4))
+    ts(B("PF", 2, 3), B("PI", 3, 4), 768, OP.add)
+    cp(B("PF", 3, 4), B("PI", 4, 5))
+    cp(B("PF", 4, 5), B("PI", 3, 4))
+    fill(B("SCP", 0, E), 0.0)
+    cp(B("LSU"), B("LST"))
+
+    def table(q, k):
+        for x in range(2):
+            o, l = 768 * k + E * x, 48 * k + 24 * x
+            (cp if q == "v" else act)(B("TAB", o, o + E), B("IOTA", E * x, E * x + E, ix=B("LSU", l, l + 24)))
+
+    def ends(buf, k):
+        return B(buf, 64 * k + 15, 64 * k + 64, 16)
+
+    def gather_ends(k):
+        tt(B("GT"), B("TAB", 768 * k, 768 * k + 768, ix=B("OFG", 4 * k, 4 * k + 4)), B("MASK"), OP.mult)
+        scan(B("SCN", 64 * k, 64 * k + 64), B("RM"), B("GT"), OP.mult, OP.add)
+        cp(B("OFW", 4 * k, 4 * k + 4), ends("SCN", k))
+
+    def diff(k):
+        tt(B("ZB", 4 * k, 4 * k + 4), ends("SCN", k), B("STB", 4 * k, 4 * k + 4), OP.subtract)
+
+    table("v", 0)
+    gather_ends(0)
+    diff(0)
+    for b in range(4):
+        cp(B("EB", 512 * b + b, 512 * b + 512, 4), B("IDN"))
+    quant("QE", "SE", 0, 512, "EB")
+    table("v", 1)
+    for b in range(4):
+        fill(B("DW", PW * b, PW * b + 1), 0.0)
+    for t in range(R):
+        fill(B("CELL%d" % t), 0.0)
+    cp(B("REP"), B("RPI"))
+    ts(B("REV"), B("RVI"), B("PF", 4, 5)[0], OP.subtract)
+    table("v", 2)
+    table("s", 3)
+
+    def lists_out(k0, sem, qs):
+        a, z = 64 * k0 + 15, 64 * k0 + 256
+        tt(B("PB", 4 * k0, 4 * k0 + 16), B("CS", a, z, 16), B("SCN", a, z, 16), OP.mult)
+        for j in range(2):
+            ts(B("PR", 2 * k0 + j, 2 * k0 + 8, 2), B("PB", 4 * k0 + 2 + j, 4 * k0 + 16, 4), -float(E), OP.add, 0.0, OP.max)
+        for j in range(2):
+            tt(B("NB", 2 * k0 + j, 2 * k0 + 8, 2), B("PR", 2 * k0 + j, 2 * k0 + 8, 2), B("PB", 4 * k0 + j, 4 * k0 + 16, 4), OP.add)
+        cp(B("NU", 2 * k0, 2 * k0 + 8), B("NB", 2 * k0, 2 * k0 + 8))
+        for i in range(4):
+            k = k0 + i
+            dma(qs[i], sem, B("OFN", p=(16 * k, 16 * k + 16)), B("NU", 2 * k, 2 * k + 2))
+
+    for t in range(R):
+        last = t == R - 1
+        for k in range(8):
+            score(k, C, E)
+            if t == 0 and 3 <= k < 7:
+                table("s", k + 1)
+        for b in range(4):
+            act(B("VP", E * b, E * b + E), mm("QE", "SE", 128 * b, "QX", "SX", 0, E))
+        for k in range(8):
+            if k:
+                gather_ends(k)
+            o, f = E * k, 64 * k
+            tt(B("GB"), B("SCP", o, o + 2 * E, ix=B("OFW", 4 * k + 2, 4 * k + 4)), B("MINM"), OP.min)
+            if 0 < k < 7:
+                diff(k)
+            tt(B("GA"), B("SCP", o + E, o + 2 * E, ix=B("OFW", 4 * k, 4 * k + 2)), B("GB"), OP.is_le)
+            scan(B("CS", f, f + 32), B("RM", 0, 32), B("GA"), OP.mult, OP.add)
+            ts(B("CS", f + 47, f + 64, 16), B("CS", f + 15, f + 32, 16), -1.0, OP.mult, 1.0, OP.add)
+            if k < 7:
+                tt(B("CZ"), ends("CS", k), B("ZB", 4 * k, 4 * k + 4), OP.mult)
+                tt(B("STB", 4 * k + 4, 4 * k + 8), B("STB", 4 * k, 4 * k + 4), B("CZ"), OP.add)
+                cp(B("OFG", 4 * k + 4, 4 * k + 8), B("STB", 4 * k + 4, 4 * k + 8))
+            if k == 4:
+                lists_out(0, "exa", "yyyy")
+        lists_out(4, "exb", "ysys")
+        if t == 0:
+            quant("QV", "SV", 0, 128, "VIN")
+        for b in (0, 2, 1, 3):
+            (cp if b < 2 else act)(B("M", b, 1024, 4), B("VP", E * b, E * b + E, ix=B("OFN")))
+        quant("QM", "SM", 0, C, "M")
+        act(B("UNW"), B("IOTA", 0, E, ix=B("OFN")))
+        cp(B("NI"), B("OFN"))
+        ts(B("T1"), B("NI"), 0x1F0, OP.bitwise_and)
+        tt(B("CEA"), B("NI"), B("T1"), OP.add)
+        tt(B("EE"), B("NI", ix=B("REP")), B("UNW"), OP.is_equal)
+        scan(B("DS"), B("EE"), B("CDG"), OP.max, OP.mult)
+        ts(B("FLB"), B("DS", 15, 256, 16), B("PF", 2, 3)[0], OP.mult)
+        tt(B("MXB"), B("CEA"), B("FLB"), OP.max)
+        ts(B("OFS", 0, 32, 2), B("MXB"), B("PF", 3, 4)[0], OP.add)
+        cell = "CELL%d" % t
+
+        def scatter(w):
+            cp(B(cell, ix=B("OFS", 2 * w, 2 * w + 1)), B("POS", 16 * w, 16 * w + 16))
+
+        for w in range(PRE):
+            scatter(w)
+        for b in range(4):
+            act(B("TT", b, 1024, 4), mm("WQ", "WS", 128 * b, "QM", "SM", 0, C), scale=0.03125)
+        quant("QT", "SQ", 0, C, "TT")
+        for b in range(4):
+            act(B("DW", PW * b + 1, PW * b + 257), mm("QE", "SE", 128 * b, "QT", "SQ", 0, C), scale=-1.0)
+        for w in range(PRE, 16):
+            scatter(w)
+        run("v", v.transpose, B("CT"), B(cell, 0, 768))
+        tt(B("CM"), B("CT", 0, 768, 32), B("CT", 16, 768, 32), OP.max)
+        cp(B("OFC"), B("CM"))
+
+        def taken(b, w0, w1):
+            return B("DW", PW * b, PW * b + 257, ix=B("OFC", w0, w1))
+
+        for b in (0, 2, 1, 3):
+            if b < 2:
+                ts(B("UB", b, 512, 4), taken(b, 16, 24), -1.0, OP.mult)
+            else:
+                act(B("UB", b, 512, 4), taken(b, 16, 24), scale=-1.0)
+        quant("QB", "SB", 0, 128, "UB")
+        exchange(nxt, prv, ((B("LB", bit=dt.uint8), B("QB", bit=dt.uint8)), (B("LS"), B("SB"))), "bar", "sbar")
+        for b in range(4):
+            tt(B("X", 512 + b, 1024, 4), taken(b, 8, 16), B("VP", E * b + H, E * b + C), OP.add)
+        quant("QX", "SX", H, C, "X")
+        for b in range(4):
+            tt(B("FU", H * b, H * b + H), taken(b, 0, 8), B("VP", E * b, E * b + H), OP.add)
+
+        def result(a, b):
+            act(B("YO", a, b), mm("QV", "SV", 0, "QX", "SX", a, b))
+            sem = "outs" if a else "oute"
+            dma("y", sem, T.oc[:, 4 * a:4 * b], B("QX", a, b, bit=dt.uint8))
+            for k in range(4):
+                dma("s" if a == 0 and k % 2 else "y", sem, T.osc[4 * k:4 * k + 4, a:b], B("SX", a, b, p=(32 * k, 32 * k + 4)))
+            dma("s", sem, T.y[:, a:b], B("YO", a, b))
+
+        if last:
+            act(B("ONR"), B("UNW", ix=B("REV")))
+            order("y", B("ONR")[1], [])
+            dma("y", "outs", T.on[:], (T.ONR[0:128:16, :], B("ONR")[1]))
+            result(H, C)
+        else:
+            for k in range(EARLY):
+                score(k, H, C)
+        for b in range(4):
+            tt(B("X", b, 512, 4), B("FU", H * b, H * b + H), mm("QE", "SE", 128 * b, "LB", "LS", 0, H), OP.subtract)
+        quant("QX", "SX", 0, H, "X")
+        if last:
+            result(0, H)
+        else:
+            send_border()
+            for k in range(8):
+                score(k, 0, H if k < EARLY else C)
+    for sem in SEMAPHORES:
+        wait("g", sem, count[sem])

@@ -12,8 +12,8 @@ LISTS = ("float8_e4m3fn_x4 QX 384 QU 128 UQ 1024 QV 128 WQ 512 QE 512 QM 256 QT 
          "bfloat16 X 1024 UIN 512 VIN 512 ONES 128 IDN 128 EB 2048 VP 1536 M 1024 TT 1024 DW 1088 CELL0 800 CELL1 800 "
          "CELL2 800 POS 256 CT 768 UB 512",
          "float32 IOTA 768 TAB 6144 SCP 3456 STB 36 SCN 512 CS 512 GT 64 GB 32 GA 32 ZB 32 CZ 4 PB 32 PR 16 NB 16 UNW 256 "
-         "CEA 16 EE 256 DS 256 FLB 16 MXB 16 CM 24 FU 512 MASK 64 MINM 32 RM 64 CDG 256 PF 8 YO 256 ONR 256",
-         "int32 LST 384 NI 16 T1 16 MD 256 MDA 256 MI 64 PI 8 UOI 64 RPI 16 RVI 16",
+         "CEA 16 EE 256 DS 256 FLB 16 MXB 16 CM 24 FU 512 MASK 64 MINM 32 RM 64 CDG 256 PF 8 YO 256 ONR 256 AB 4",
+         "int32 LST 384 NI 16 T1 16 MD 256 MDA 256 MI 64 MJ 64 PI 8 UOI 64",
          "uint16 LSU 384 OFG 32 OFW 32 NU 16 OFN 16 OFS 32 OFC 24 UOF 64 REP 16 REV 16")
 WIDTH = {}
 SCRATCH = {}
@@ -57,7 +57,7 @@ def rank_program(g, core, T, topo):
 
     def order(q, reads, writes):
         need = {}
-        for kinds, regs in (("w", reads), ("rw", writes)):
+        for kinds, regs in (("wW", reads), ("rw", writes)):
             for n, p0, p1, c0, c1, st in regs:
                 for k, a0, a1, b0, b1, su, sem, val, far in log.get(n, ()):
                     if k in kinds and a0 < p1 and p0 < a1 and b0 < c1 and c0 < b1 and (st != su or (c0 - b0) % st == 0):
@@ -69,6 +69,10 @@ def rank_program(g, core, T, topo):
         for n, p0, p1, c0, c1, st in writes:
             log[n] = [x for x in log.get(n, ()) if not (p0 <= x[1] and x[2] <= p1 and c0 <= x[3] and x[4] <= c1
                                                         and (st == 1 or st == x[5] and (c0 - x[3]) % st == 0))]
+        for n, p0, p1, c0, c1, st in reads:
+            if st == 1:
+                log[n] = [("W",) + x[1:] if x[0] == "w" and p0 <= x[1] and x[2] <= p1 and c0 <= x[3] and x[4] <= c1 else x
+                          for x in log.get(n, ())]
         for kind, regs in (("w", writes), ("r", reads)):
             for r in regs:
                 log.setdefault(r[0], []).append((kind,) + r[1:] + (sem, count[sem], far))
@@ -145,22 +149,21 @@ def rank_program(g, core, T, topo):
     def send_border():
         exchange(prv, nxt, ((B("QX", C, E, bit=dt.uint8), B("QX", 0, H, bit=dt.uint8)), (B("SX", C, E), B("SX", 0, H))), "brd", "sbrd")
 
-    def iota(out, pattern, base, cm):
-        run("g", g.iota, out, pattern, base, cm, allow_small_or_imprecise_dtypes=True)
-
     dma("y", "lx0", B("X", 0, 512), T.x[:, 0:512])
-    dma("s", "lx1", B("X", 512, 1024), T.x[:, 512:1024])
-    dma("y", "lu", B("UIN"), T.u[:])
+    dma("s", "lu", B("UIN"), T.u[:])
     for k in range(8):
         dma("y", "la", B("LST", 48 * k, 48 * k + 24, p=(0, 16)), T.lf[16 * k:16 * k + 16, :])
         dma("s", "lb", B("LST", 48 * k + 24, 48 * k + 48, p=(0, 16)), T.rt[16 * k:16 * k + 16, :])
+    dma("y", "lx1", B("X", 512, 1024), T.x[:, 512:1024])
+    run("g", g.iota, B("IOTA", 0, E), [[1, E]], 0, 0, allow_small_or_imprecise_dtypes=True)
+    run("g", g.iota, B("PI", 0, 1), [[1, 1]], 0, 1)
     fill(B("ONES"), 1.0)
-    fill(B("EB"), 0.0)
     run("g", g.affine_select, B("IDN"), B("ONES"), [[-1, 128]], OP.is_equal, 0.0, 0, 1)
-    iota(B("UOI"), [[16, 8], [0, 8]], 0, 0)
-    iota(B("MD"), [[1, 256]], 256, -1)
-    iota(B("PI", 0, 1), [[1, 1]], 0, 1)
-    iota(B("MI"), [[1, 64]], 0, 0)
+    fill(B("EB"), 0.0)
+    cp(B("MI"), B("IOTA", 0, 64))
+    ts(B("UOI"), B("MI"), 0x38, OP.bitwise_and)
+    ts(B("UOF"), B("UOI"), 2, OP.mult)
+    cp(B("PF", 0, 1), B("PI", 0, 1))
     quant("QX", "SX", 0, H, "X")
     send_border()
     dma("s", "lwc", B("WQ", bit=dt.uint8), T.wc[:])
@@ -168,35 +171,28 @@ def rank_program(g, core, T, topo):
     for h in range(1, 8):
         dma("y", "lr", B("LST", p=(16 * h, 16 * h + 16)), B("LST", p=(0, 16)))
     dma("y", "lv", B("VIN"), T.v[:])
-    iota(B("IOTA"), [[1, 768]], 0, 0)
-    iota(B("POS"), [[1, 256]], 1, 0)
-    iota(B("RPI"), [[1, 16]], 0, 0)
-    iota(B("RVI"), [[-16, 16]], 255, 0)
-    quant("QX", "SX", H, C, "X")
-    cp(B("UOF"), B("UOI"))
     quant("QU", "SU", 0, 128, "UIN")
     cp(B("UQ", bit=dt.uint32), B("QU", bit=dt.uint32, ix=B("UOF")))
     act(B("US"), B("SU", ix=B("UOF")))
+    quant("QX", "SX", H, C, "X")
     for k in range(8):
         score(k, 0, C)
+    ts(B("MD"), B("IOTA", 0, 256), B("PF", 0, 1), OP.subtract, 256.0, OP.add)
     ts(B("MDA"), B("MD"), 15, OP.bitwise_and)
     ts(B("MASK"), B("MDA", 0, 64), 0, OP.is_equal)
     ts(B("MINM"), B("MASK", 0, 32), 1e29, OP.mult, -1.0, OP.add)
-    ts(B("CDG"), B("MDA"), 0, OP.not_equal)
-    ts(B("MI"), B("MI"), 15, OP.bitwise_and)
-    ts(B("RM"), B("MI"), 0, OP.not_equal)
+    ts(B("MJ"), B("MI"), 15, OP.bitwise_and)
+    ts(B("RM"), B("MJ"), 0, OP.not_equal)
     ts(B("PI", 1, 2), B("PI", 0, 1), 7, OP.bitwise_and)
     ts(B("PI", 2, 3), B("PI", 0, 1), 3, OP.arith_shift_right)
     ts(B("PI", 3, 4), B("PI", 0, 1), 15, OP.bitwise_and)
     ts(B("PI", 4, 5), B("PI", 0, 1), 16, OP.bitwise_and)
-    ts(B("PF", 0, 1), B("PI", 1, 2), 32, OP.mult)
-    tt(B("PF", 1, 2), B("PF", 0, 1), B("PI", 2, 3), OP.add)
+    ts(B("PF", 5, 6), B("PI", 1, 2), 32, OP.mult)
+    tt(B("PF", 1, 2), B("PF", 5, 6), B("PI", 2, 3), OP.add)
     for x in range(4):
         ts(B("STB", x, x + 1), B("PF", 1, 2), -1.0, OP.mult, float(255 - 16 * (x % 2) + E * (x // 2)), OP.add)
     cp(B("OFG", 0, 4), B("STB", 0, 4))
-    ts(B("PF", 2, 3), B("PI", 3, 4), 768, OP.add)
-    cp(B("PF", 3, 4), B("PI", 4, 5))
-    cp(B("PF", 4, 5), B("PI", 3, 4))
+    ts(B("IOTA", E, 2 * E), B("IOTA", 0, E), float(E), OP.add)
     fill(B("SCP", 0, E), 0.0)
     cp(B("LSU"), B("LST"))
 
@@ -208,48 +204,70 @@ def rank_program(g, core, T, topo):
     def ends(buf, k):
         return B(buf, 64 * k + 15, 64 * k + 64, 16)
 
+    def col(buf, x):
+        return B(buf, x, x + 1)
+
     def gather_ends(k):
         tt(B("GT"), B("TAB", 768 * k, 768 * k + 768, ix=B("OFG", 4 * k, 4 * k + 4)), B("MASK"), OP.mult)
+        spare()
         scan(B("SCN", 64 * k, 64 * k + 64), B("RM"), B("GT"), OP.mult, OP.add)
+        spare()
         cp(B("OFW", 4 * k, 4 * k + 4), ends("SCN", k))
+        spare()
 
     def diff(k):
         tt(B("ZB", 4 * k, 4 * k + 4), ends("SCN", k), B("STB", 4 * k, 4 * k + 4), OP.subtract)
 
+    todo = []
+
+    def spare():
+        if todo:
+            todo.pop(0)()
+
     table("v", 0)
     gather_ends(0)
     diff(0)
+    table("v", 1)
+    table("s", 2)
     for b in range(4):
         cp(B("EB", 512 * b + b, 512 * b + 512, 4), B("IDN"))
     quant("QE", "SE", 0, 512, "EB")
-    table("v", 1)
     for b in range(4):
-        fill(B("DW", PW * b, PW * b + 1), 0.0)
+        todo.append(lambda b=b: fill(B("DW", PW * b, PW * b + 1), 0.0))
     for t in range(R):
-        fill(B("CELL%d" % t), 0.0)
-    cp(B("REP"), B("RPI"))
-    ts(B("REV"), B("RVI"), B("PF", 4, 5)[0], OP.subtract)
-    table("v", 2)
-    table("s", 3)
+        todo.append(lambda t=t: fill(B("CELL%d" % t), 0.0))
+    todo.append(lambda: ts(B("CDG"), B("MDA"), 0, OP.not_equal))
+    todo.append(lambda: ts(B("PF", 2, 3), B("PI", 3, 4), 768, OP.add))
+    todo.append(lambda: cp(B("PF", 3, 4), B("PI", 4, 5)))
+    todo.append(lambda: ts(B("PF", 4, 5), B("PI", 3, 4), -1.0, OP.mult, 255.0, OP.add))
+    todo.append(lambda: ts(B("POS"), B("IOTA", 0, 256), 1.0, OP.add))
+    todo.append(lambda: cp(B("REP"), B("IOTA", 0, 16)))
+    todo.append(lambda: ts(B("REV"), B("IOTA", 0, 16), -16.0, OP.mult, B("PF", 4, 5)[0], OP.add))
+    todo.append(lambda: quant("QV", "SV", 0, 128, "VIN"))
 
-    def lists_out(k0, sem, qs):
-        a, z = 64 * k0 + 15, 64 * k0 + 256
-        tt(B("PB", 4 * k0, 4 * k0 + 16), B("CS", a, z, 16), B("SCN", a, z, 16), OP.mult)
+    def lists_out(k0, k1, sem):
+        a, z, x, y = 64 * k0 + 15, 64 * k1, 4 * k0, 4 * k1
+        todo.append(lambda: tt(B("PB", x, y), B("CS", a, z, 16), B("SCN", a, z, 16), OP.mult))
         for j in range(2):
-            ts(B("PR", 2 * k0 + j, 2 * k0 + 8, 2), B("PB", 4 * k0 + 2 + j, 4 * k0 + 16, 4), -float(E), OP.add, 0.0, OP.max)
+            todo.append(lambda j=j: ts(B("PR", 2 * k0 + j, 2 * k1, 2), B("PB", x + 2 + j, y, 4), -float(E), OP.add, 0.0, OP.max))
         for j in range(2):
-            tt(B("NB", 2 * k0 + j, 2 * k0 + 8, 2), B("PR", 2 * k0 + j, 2 * k0 + 8, 2), B("PB", 4 * k0 + j, 4 * k0 + 16, 4), OP.add)
-        cp(B("NU", 2 * k0, 2 * k0 + 8), B("NB", 2 * k0, 2 * k0 + 8))
-        for i in range(4):
-            k = k0 + i
-            dma(qs[i], sem, B("OFN", p=(16 * k, 16 * k + 16)), B("NU", 2 * k, 2 * k + 2))
+            todo.append(lambda j=j: tt(B("NB", 2 * k0 + j, 2 * k1, 2), B("PR", 2 * k0 + j, 2 * k1, 2), B("PB", x + j, y, 4), OP.add))
+
+        def end():
+            cp(B("NU", 2 * k0, 2 * k1), B("NB", 2 * k0, 2 * k1))
+            for k in range(k0, k1):
+                list_out(k, sem)
+        todo.append(end)
+
+    def list_out(k, sem):
+        dma("y", sem, B("OFN", p=(16 * k, 16 * k + 16)), B("NU", 2 * k, 2 * k + 2))
 
     for t in range(R):
         last = t == R - 1
         for k in range(8):
             score(k, C, E)
-            if t == 0 and 3 <= k < 7:
-                table("s", k + 1)
+            if t == 0 and 1 <= k < 6:
+                table("s", k + 2)
         for b in range(4):
             act(B("VP", E * b, E * b + E), mm("QE", "SE", 128 * b, "QX", "SX", 0, E))
         for k in range(8):
@@ -259,18 +277,33 @@ def rank_program(g, core, T, topo):
             tt(B("GB"), B("SCP", o, o + 2 * E, ix=B("OFW", 4 * k + 2, 4 * k + 4)), B("MINM"), OP.min)
             if 0 < k < 7:
                 diff(k)
+            if k == 7:
+                ts(B("AB", 0, 2), B("SCN", f + 47, f + 64, 16), -float(E), OP.add)
             tt(B("GA"), B("SCP", o + E, o + 2 * E, ix=B("OFW", 4 * k, 4 * k + 2)), B("GB"), OP.is_le)
+            if k == 7:
+                tt(B("AB", 2, 4), B("SCN", f + 15, f + 32, 16), B("AB", 0, 2), OP.subtract)
+            spare()
             scan(B("CS", f, f + 32), B("RM", 0, 32), B("GA"), OP.mult, OP.add)
-            ts(B("CS", f + 47, f + 64, 16), B("CS", f + 15, f + 32, 16), -1.0, OP.mult, 1.0, OP.add)
+            spare()
             if k < 7:
+                ts(B("CS", f + 47, f + 64, 16), B("CS", f + 15, f + 32, 16), -1.0, OP.mult, 1.0, OP.add)
+                spare()
                 tt(B("CZ"), ends("CS", k), B("ZB", 4 * k, 4 * k + 4), OP.mult)
+                spare()
                 tt(B("STB", 4 * k + 4, 4 * k + 8), B("STB", 4 * k, 4 * k + 4), B("CZ"), OP.add)
+                spare()
                 cp(B("OFG", 4 * k + 4, 4 * k + 8), B("STB", 4 * k + 4, 4 * k + 8))
-            if k == 4:
-                lists_out(0, "exa", "yyyy")
-        lists_out(4, "exb", "ysys")
-        if t == 0:
-            quant("QV", "SV", 0, 128, "VIN")
+                spare()
+            else:
+                while todo:
+                    spare()
+                for j in range(2):
+                    ts(col("NU", 14 + j), col("CS", f + 15 + 16 * j), col("AB", 2 + j), OP.mult, col("AB", j), OP.add)
+                list_out(7, "exb")
+            if k == 3:
+                lists_out(0, 4, "exa")
+            if k == 6:
+                lists_out(4, 7, "exb")
         for b in (0, 2, 1, 3):
             (cp if b < 2 else act)(B("M", b, 1024, 4), B("VP", E * b, E * b + E, ix=B("OFN")))
         quant("QM", "SM", 0, C, "M")
@@ -280,9 +313,9 @@ def rank_program(g, core, T, topo):
         tt(B("CEA"), B("NI"), B("T1"), OP.add)
         tt(B("EE"), B("NI", ix=B("REP")), B("UNW"), OP.is_equal)
         scan(B("DS"), B("EE"), B("CDG"), OP.max, OP.mult)
-        ts(B("FLB"), B("DS", 15, 256, 16), B("PF", 2, 3)[0], OP.mult)
+        ts(B("FLB"), B("DS", 15, 256, 16), B("PF", 2, 3), OP.mult)
         tt(B("MXB"), B("CEA"), B("FLB"), OP.max)
-        ts(B("OFS", 0, 32, 2), B("MXB"), B("PF", 3, 4)[0], OP.add)
+        ts(B("OFS", 0, 32, 2), B("MXB"), B("PF", 3, 4), OP.add)
         cell = "CELL%d" % t
 
         def scatter(w):
@@ -327,7 +360,6 @@ def rank_program(g, core, T, topo):
 
         if last:
             act(B("ONR"), B("UNW", ix=B("REV")))
-            order("y", B("ONR")[1], [])
             dma("y", "outs", T.on[:], (T.ONR[0:128:16, :], B("ONR")[1]))
             result(H, C)
         else:

@@ -3,18 +3,16 @@ from concourse.mybir import dt, AluOpType, ActivationFunctionType
 OP = AluOpType
 AF = ActivationFunctionType
 N, R, C, H, E = 8, 3, 256, 128, 384
-CW = 800
 PW = 272
 EARLY = 4
-PRE = 4
 LISTS = ("float8_e4m3fn_x4 QX 384 QU 128 UQ 1024 QV 128 WQ 512 QE 512 QM 256 QT 256 QB 128 LB 128",
          "uint8 SX 384 SU 128 US 1024 SV 128 WS 512 SE 512 SM 256 SQ 256 SB 128 LS 128",
-         "bfloat16 X 1024 UIN 512 VIN 512 ONES 128 IDN 128 EB 2048 VP 1536 M 1024 TT 1024 DW 1088 CELL0 800 CELL1 800 "
-         "CELL2 800 POS 256 CT 768 UB 512",
-         "float32 IOTA 768 TAB 6144 SCP 3456 STB 36 SCN 512 CS 512 GT 64 GB 32 GA 32 ZB 32 CZ 4 PB 32 PR 16 NB 16 UNW 256 "
-         "CEA 16 EE 256 DS 256 FLB 16 MXB 16 CM 24 FU 512 MASK 64 MINM 32 RM 64 CDG 256 PF 8 YO 256 ONR 256 AB 4",
-         "int32 LST 384 NI 16 T1 16 MD 256 MDA 256 MI 64 MJ 64 PI 8 UOI 64",
-         "uint16 LSU 384 OFG 32 OFW 32 NU 16 OFN 16 OFS 32 OFC 24 UOF 64 REP 16 REV 16")
+         "bfloat16 X 1024 UIN 512 VIN 512 ONES 512 EB 2048 VP 1536 M 1024 TT 1024 DW 1088 CELL0 816 CELL1 816 "
+         "CELL2 816 POS 256 CT 768 UB 512",
+         "float32 IOTA 768 TAB 6144 SCP 3456 STB 36 SCN 512 CS 256 GT 64 GB 32 GA 32 ZB 32 BU 16 AB 16 FA 16 NB 16 UNW 256 "
+         "CEA 16 EE 512 DS 512 FLB 16 MXB 16 CM 24 FU 512 MASK 64 MINM 32 RM 64 CDG 512 PF 8 YO 256 ONR 256",
+         "int32 LST 384 NI 16 T1 16 MD 64 MDA 64 ME 512 MF 512 MI 64 MJ 64 PI 8 UOI 64 RI 32",
+         "uint16 LSU 384 OFG 32 OFW 32 NU 16 OFN 16 OFS 16 OFC 24 UOF 64 REP 32 REV 16")
 WIDTH = {}
 SCRATCH = {}
 for _line in LISTS:
@@ -25,8 +23,8 @@ for _line in LISTS:
 for _i in range(8):
     WIDTH["ps%d" % _i] = 512
     SCRATCH["ps%d" % _i] = ("psum", [128, 512], "float32")
-SEMAPHORES = ["v", "s", "pe", "gp", "lx0", "lx1", "lu", "lv", "lwc", "lws", "la", "lb", "lr", "exa", "exb", "outs", "oute",
-              "brd", "bar", "sbrd", "sbar"]
+SEMAPHORES = ["v", "s", "pe", "gp", "lx0", "lx1", "lu", "lv", "lwc", "lws", "la", "lb", "lr", "exa", "exb", "exc", "outs",
+              "oute", "brd", "bar", "sbrd", "sbar"]
 
 
 def rank_program(g, core, T, topo):
@@ -131,6 +129,9 @@ def rank_program(g, core, T, topo):
     def fill(x, c):
         run("v", v.memset, x, c)
 
+    def iota(out, n, base, cm):
+        run("g", g.iota, out, [[1, n]], base, cm, allow_small_or_imprecise_dtypes=True)
+
     def quant(q, sc, a, b, tile):
         run("v", v.quantize_mx, B(q, a, b), B(sc, a, b), B(tile, 4 * a, 4 * b), outs=2)
 
@@ -149,27 +150,38 @@ def rank_program(g, core, T, topo):
     def send_border():
         exchange(prv, nxt, ((B("QX", C, E, bit=dt.uint8), B("QX", 0, H, bit=dt.uint8)), (B("SX", C, E), B("SX", 0, H))), "brd", "sbrd")
 
+    soon, todo = [], []
+
+    def spare():
+        if soon or todo:
+            (soon or todo).pop(0)()
+
+    def later(f, *a, to=todo):
+        to.append(lambda: f(*a))
+
     dma("y", "lx0", B("X", 0, 512), T.x[:, 0:512])
     dma("s", "lu", B("UIN"), T.u[:])
     for k in range(8):
         dma("y", "la", B("LST", 48 * k, 48 * k + 24, p=(0, 16)), T.lf[16 * k:16 * k + 16, :])
         dma("s", "lb", B("LST", 48 * k + 24, 48 * k + 48, p=(0, 16)), T.rt[16 * k:16 * k + 16, :])
     dma("y", "lx1", B("X", 512, 1024), T.x[:, 512:1024])
-    run("g", g.iota, B("IOTA", 0, E), [[1, E]], 0, 0, allow_small_or_imprecise_dtypes=True)
-    run("g", g.iota, B("PI", 0, 1), [[1, 1]], 0, 1)
+    for h in range(1, 8):
+        dma("y", "lr", B("LST", p=(16 * h, 16 * h + 16)), B("LST", p=(0, 16)))
+    iota(B("IOTA", 0, E), E, 0, 0)
+    iota(B("PI", 0, 1), 1, 0, 1)
+    iota(B("IOTA", E, 2 * E), E, E, 0)
     fill(B("ONES"), 1.0)
-    run("g", g.affine_select, B("IDN"), B("ONES"), [[-1, 128]], OP.is_equal, 0.0, 0, 1)
-    fill(B("EB"), 0.0)
     cp(B("MI"), B("IOTA", 0, 64))
     ts(B("UOI"), B("MI"), 0x38, OP.bitwise_and)
     ts(B("UOF"), B("UOI"), 2, OP.mult)
     cp(B("PF", 0, 1), B("PI", 0, 1))
     quant("QX", "SX", 0, H, "X")
     send_border()
+    iota(B("SCP", 0, E), E, 0, 0)
+    for b in range(4):
+        run("g", g.affine_select, B("EB", 512 * b, 512 * b + 512), B("ONES"), [[-8, 128], [-1, 4]], OP.is_equal, 0.0, b, 8)
     dma("s", "lwc", B("WQ", bit=dt.uint8), T.wc[:])
     dma("s", "lws", B("WS"), T.ws[:])
-    for h in range(1, 8):
-        dma("y", "lr", B("LST", p=(16 * h, 16 * h + 16)), B("LST", p=(0, 16)))
     dma("y", "lv", B("VIN"), T.v[:])
     quant("QU", "SU", 0, 128, "UIN")
     cp(B("UQ", bit=dt.uint32), B("QU", bit=dt.uint32, ix=B("UOF")))
@@ -177,32 +189,25 @@ def rank_program(g, core, T, topo):
     quant("QX", "SX", H, C, "X")
     for k in range(8):
         score(k, 0, C)
-    ts(B("MD"), B("IOTA", 0, 256), B("PF", 0, 1), OP.subtract, 256.0, OP.add)
-    ts(B("MDA"), B("MD"), 15, OP.bitwise_and)
-    ts(B("MASK"), B("MDA", 0, 64), 0, OP.is_equal)
-    ts(B("MINM"), B("MASK", 0, 32), 1e29, OP.mult, -1.0, OP.add)
-    ts(B("MJ"), B("MI"), 15, OP.bitwise_and)
-    ts(B("RM"), B("MJ"), 0, OP.not_equal)
+    ts(B("MD"), B("IOTA", 0, 64), B("PF", 0, 1), OP.subtract, 256.0, OP.add)
     ts(B("PI", 1, 2), B("PI", 0, 1), 7, OP.bitwise_and)
+    ts(B("MDA"), B("MD"), 15, OP.bitwise_and)
     ts(B("PI", 2, 3), B("PI", 0, 1), 3, OP.arith_shift_right)
-    ts(B("PI", 3, 4), B("PI", 0, 1), 15, OP.bitwise_and)
-    ts(B("PI", 4, 5), B("PI", 0, 1), 16, OP.bitwise_and)
+    ts(B("MASK"), B("MDA"), 0, OP.is_equal)
     ts(B("PF", 5, 6), B("PI", 1, 2), 32, OP.mult)
+    ts(B("MINM"), B("MASK", 0, 32), 1e29, OP.mult, -1.0, OP.add)
     tt(B("PF", 1, 2), B("PF", 5, 6), B("PI", 2, 3), OP.add)
+    ts(B("MJ"), B("MI"), 15, OP.bitwise_and)
     for x in range(4):
         ts(B("STB", x, x + 1), B("PF", 1, 2), -1.0, OP.mult, float(255 - 16 * (x % 2) + E * (x // 2)), OP.add)
+    ts(B("RM"), B("MJ"), 0, OP.not_equal)
     cp(B("OFG", 0, 4), B("STB", 0, 4))
-    ts(B("IOTA", E, 2 * E), B("IOTA", 0, E), float(E), OP.add)
-    fill(B("SCP", 0, E), 0.0)
     cp(B("LSU"), B("LST"))
 
     def table(q, k):
         for x in range(2):
             o, l = 768 * k + E * x, 48 * k + 24 * x
             (cp if q == "v" else act)(B("TAB", o, o + E), B("IOTA", E * x, E * x + E, ix=B("LSU", l, l + 24)))
-
-    def ends(buf, k):
-        return B(buf, 64 * k + 15, 64 * k + 64, 16)
 
     def col(buf, x):
         return B(buf, x, x + 1)
@@ -212,94 +217,109 @@ def rank_program(g, core, T, topo):
         spare()
         scan(B("SCN", 64 * k, 64 * k + 64), B("RM"), B("GT"), OP.mult, OP.add)
         spare()
-        cp(B("OFW", 4 * k, 4 * k + 4), ends("SCN", k))
+        cp(B("OFW", 4 * k, 4 * k + 4), B("SCN", 64 * k + 15, 64 * k + 64, 16))
         spare()
 
-    def diff(k):
-        tt(B("ZB", 4 * k, 4 * k + 4), ends("SCN", k), B("STB", 4 * k, 4 * k + 4), OP.subtract)
-
-    todo = []
-
-    def spare():
-        if todo:
-            todo.pop(0)()
+    def diff(k, x):
+        n = 4 * k + 2 * x
+        w, o = B("SCN", 64 * k + 15 + 32 * x, 64 * k + 32 + 32 * x, 16), B("STB", n, n + 2)
+        tt(B("ZB", n, n + 2), *((o, w) if x else (w, o)), OP.subtract)
 
     table("v", 0)
     gather_ends(0)
-    diff(0)
-    table("v", 1)
-    table("s", 2)
+    diff(0, 0)
+    diff(0, 1)
+    later(ts, B("PI", 3, 4), B("PI", 0, 1), 15, OP.bitwise_and)
+    later(ts, B("PI", 4, 5), B("PI", 0, 1), 16, OP.bitwise_and)
+    later(fill, B("CELL0"), 0.0)
+    later(cp, B("PF", 4, 5), B("PI", 3, 4))
+    later(cp, B("PF", 3, 4), B("PI", 4, 5))
+    later(ts, B("PF", 2, 3), B("PI", 3, 4), 768, OP.add)
+    later(ts, B("PF", 6, 7), B("PI", 3, 4), 784, OP.add)
+    later(quant, "QE", "SE", 0, 512, "EB")
+    for x in range(2):
+        later(ts, B("ME", 256 * x, 256 * x + 256), B("IOTA", 0, 256), B("PF", 4, 5), OP.subtract, 256.0 - 16 * x, OP.add)
+        later(ts, B("RI", 16 * x, 16 * x + 16), B("MI", 0, 16), 14, OP.bitwise_and)
+    later(ts, B("MF"), B("ME"), 31, OP.bitwise_and)
+    for x in range(2):
+        later(ts, B("REP", 16 * x, 16 * x + 16), B("RI", 16 * x, 16 * x + 16), x, OP.add)
+    later(ts, B("CDG"), B("MF"), 0, OP.not_equal)
+    later(ts, B("PF", 7, 8), B("PF", 4, 5), -1.0, OP.mult, 255.0, OP.add)
+    later(ts, B("POS"), B("IOTA", 0, 256), 1.0, OP.add)
+    later(ts, B("REV"), B("IOTA", 0, 16), -16.0, OP.mult, B("PF", 7, 8), OP.add)
     for b in range(4):
-        cp(B("EB", 512 * b + b, 512 * b + 512, 4), B("IDN"))
-    quant("QE", "SE", 0, 512, "EB")
-    for b in range(4):
-        todo.append(lambda b=b: fill(B("DW", PW * b, PW * b + 1), 0.0))
-    for t in range(R):
-        todo.append(lambda t=t: fill(B("CELL%d" % t), 0.0))
-    todo.append(lambda: ts(B("CDG"), B("MDA"), 0, OP.not_equal))
-    todo.append(lambda: ts(B("PF", 2, 3), B("PI", 3, 4), 768, OP.add))
-    todo.append(lambda: cp(B("PF", 3, 4), B("PI", 4, 5)))
-    todo.append(lambda: ts(B("PF", 4, 5), B("PI", 3, 4), -1.0, OP.mult, 255.0, OP.add))
-    todo.append(lambda: ts(B("POS"), B("IOTA", 0, 256), 1.0, OP.add))
-    todo.append(lambda: cp(B("REP"), B("IOTA", 0, 16)))
-    todo.append(lambda: ts(B("REV"), B("IOTA", 0, 16), -16.0, OP.mult, B("PF", 4, 5)[0], OP.add))
-    todo.append(lambda: quant("QV", "SV", 0, 128, "VIN"))
+        later(fill, B("DW", PW * b, PW * b + 1), 0.0)
+    later(quant, "QV", "SV", 0, 128, "VIN")
+    for t in range(1, R):
+        later(fill, B("CELL%d" % t), 0.0)
+
+    def list_out(k, sem):
+        dma("y", sem, B("OFN", p=(16 * k, 16 * k + 16)), B("NU", 2 * k, 2 * k + 2))
 
     def lists_out(k0, k1, sem):
-        a, z, x, y = 64 * k0 + 15, 64 * k1, 4 * k0, 4 * k1
-        todo.append(lambda: tt(B("PB", x, y), B("CS", a, z, 16), B("SCN", a, z, 16), OP.mult))
-        for j in range(2):
-            todo.append(lambda j=j: ts(B("PR", 2 * k0 + j, 2 * k1, 2), B("PB", x + 2 + j, y, 4), -float(E), OP.add, 0.0, OP.max))
-        for j in range(2):
-            todo.append(lambda j=j: tt(B("NB", 2 * k0 + j, 2 * k1, 2), B("PR", 2 * k0 + j, 2 * k1, 2), B("PB", x + j, y, 4), OP.add))
+        def part(buf, j):
+            return B(buf, 2 * k0 + j, 2 * k1, 2)
 
         def end():
             cp(B("NU", 2 * k0, 2 * k1), B("NB", 2 * k0, 2 * k1))
             for k in range(k0, k1):
                 list_out(k, sem)
-        todo.append(end)
 
-    def list_out(k, sem):
-        dma("y", sem, B("OFN", p=(16 * k, 16 * k + 16)), B("NU", 2 * k, 2 * k + 2))
+        for j in range(2):
+            later(ts, part("BU", j), B("SCN", 64 * k0 + 47 + 16 * j, 64 * k1, 64), -float(E), OP.add, to=soon)
+        for j in range(2):
+            later(tt, part("AB", j), B("SCN", 64 * k0 + 15 + 16 * j, 64 * k1, 64), part("BU", j), OP.subtract, to=soon)
+        for j in range(2):
+            later(tt, part("FA", j), B("CS", 32 * k0 + 15 + 16 * j, 32 * k1, 32), part("AB", j), OP.mult, to=soon)
+        for j in range(2):
+            later(tt, part("NB", j), part("FA", j), part("BU", j), OP.add, to=soon)
+        later(end, to=soon)
 
     for t in range(R):
         last = t == R - 1
+
+        def numbers():
+            for b in range(4):
+                act(B("VP", E * b, E * b + E), mm("QE", "SE", 128 * b, "QX", "SX", 0, E))
+
+        if t == 0:
+            table("s", 1)
         for k in range(8):
             score(k, C, E)
-            if t == 0 and 1 <= k < 6:
-                table("s", k + 2)
-        for b in range(4):
-            act(B("VP", E * b, E * b + E), mm("QE", "SE", 128 * b, "QX", "SX", 0, E))
+            if t == 0 and 1 <= k < 7:
+                table("s", k + 1)
+        if t:
+            numbers()
         for k in range(8):
+            if t == 0 and k == 5:
+                numbers()
             if k:
                 gather_ends(k)
-            o, f = E * k, 64 * k
+            o, f, c, n = E * k, 64 * k, 32 * k, 4 * k + 4
             tt(B("GB"), B("SCP", o, o + 2 * E, ix=B("OFW", 4 * k + 2, 4 * k + 4)), B("MINM"), OP.min)
             if 0 < k < 7:
-                diff(k)
+                diff(k, 0)
             if k == 7:
-                ts(B("AB", 0, 2), B("SCN", f + 47, f + 64, 16), -float(E), OP.add)
+                ts(B("BU", 14, 16), B("SCN", f + 47, f + 64, 16), -float(E), OP.add)
             tt(B("GA"), B("SCP", o + E, o + 2 * E, ix=B("OFW", 4 * k, 4 * k + 2)), B("GB"), OP.is_le)
+            if 0 < k < 7:
+                diff(k, 1)
             if k == 7:
-                tt(B("AB", 2, 4), B("SCN", f + 15, f + 32, 16), B("AB", 0, 2), OP.subtract)
+                tt(B("AB", 14, 16), B("SCN", f + 15, f + 32, 16), B("BU", 14, 16), OP.subtract)
             spare()
-            scan(B("CS", f, f + 32), B("RM", 0, 32), B("GA"), OP.mult, OP.add)
+            scan(B("CS", c, c + 32), B("RM", 0, 32), B("GA"), OP.mult, OP.add)
             spare()
             if k < 7:
-                ts(B("CS", f + 47, f + 64, 16), B("CS", f + 15, f + 32, 16), -1.0, OP.mult, 1.0, OP.add)
-                spare()
-                tt(B("CZ"), ends("CS", k), B("ZB", 4 * k, 4 * k + 4), OP.mult)
-                spare()
-                tt(B("STB", 4 * k + 4, 4 * k + 8), B("STB", 4 * k, 4 * k + 4), B("CZ"), OP.add)
-                spare()
-                cp(B("OFG", 4 * k + 4, 4 * k + 8), B("STB", 4 * k + 4, 4 * k + 8))
-                spare()
+                for x in range(4):
+                    base = col("SCN", f + 15 + 16 * x) if x > 1 else col("STB", 4 * k + x)
+                    ts(col("OFG", n + x), col("CS", c + 15 + 16 * (x % 2)), col("ZB", 4 * k + x), OP.mult, base, OP.add)
+                soon.insert(0, lambda n=n: cp(B("STB", n, n + 4), B("OFG", n, n + 4)))
             else:
-                while todo:
+                while soon:
                     spare()
                 for j in range(2):
-                    ts(col("NU", 14 + j), col("CS", f + 15 + 16 * j), col("AB", 2 + j), OP.mult, col("AB", j), OP.add)
-                list_out(7, "exb")
+                    ts(col("NU", 14 + j), col("CS", c + 15 + 16 * j), col("AB", 14 + j), OP.mult, col("BU", 14 + j), OP.add)
+                list_out(7, "exc")
             if k == 3:
                 lists_out(0, 4, "exa")
             if k == 6:
@@ -307,29 +327,27 @@ def rank_program(g, core, T, topo):
         for b in (0, 2, 1, 3):
             (cp if b < 2 else act)(B("M", b, 1024, 4), B("VP", E * b, E * b + E, ix=B("OFN")))
         quant("QM", "SM", 0, C, "M")
+        while todo:
+            spare()
         act(B("UNW"), B("IOTA", 0, E, ix=B("OFN")))
         cp(B("NI"), B("OFN"))
         ts(B("T1"), B("NI"), 0x1F0, OP.bitwise_and)
+        for x in range(2):
+            tt(B("EE", 256 * x, 256 * x + 256), B("NI", ix=B("REP", 16 * x, 16 * x + 16)), B("UNW"), OP.is_equal)
         tt(B("CEA"), B("NI"), B("T1"), OP.add)
-        tt(B("EE"), B("NI", ix=B("REP")), B("UNW"), OP.is_equal)
         scan(B("DS"), B("EE"), B("CDG"), OP.max, OP.mult)
-        ts(B("FLB"), B("DS", 15, 256, 16), B("PF", 2, 3), OP.mult)
+        for x in range(2):
+            ts(B("FLB", x, 16, 2), B("DS", 256 * x + 31, 256 * x + 256, 32), B("PF", 6, 7) if x else B("PF", 2, 3), OP.mult)
         tt(B("MXB"), B("CEA"), B("FLB"), OP.max)
-        ts(B("OFS", 0, 32, 2), B("MXB"), B("PF", 3, 4), OP.add)
-        cell = "CELL%d" % t
-
-        def scatter(w):
-            cp(B(cell, ix=B("OFS", 2 * w, 2 * w + 1)), B("POS", 16 * w, 16 * w + 16))
-
-        for w in range(PRE):
-            scatter(w)
+        ts(B("OFS"), B("MXB"), B("PF", 3, 4), OP.add)
         for b in range(4):
             act(B("TT", b, 1024, 4), mm("WQ", "WS", 128 * b, "QM", "SM", 0, C), scale=0.03125)
         quant("QT", "SQ", 0, C, "TT")
         for b in range(4):
             act(B("DW", PW * b + 1, PW * b + 257), mm("QE", "SE", 128 * b, "QT", "SQ", 0, C), scale=-1.0)
-        for w in range(PRE, 16):
-            scatter(w)
+        cell = "CELL%d" % t
+        for w in range(8):
+            cp(B(cell, ix=B("OFS", 2 * w, 2 * w + 2)), B("POS", 32 * w, 32 * w + 32))
         run("v", v.transpose, B("CT"), B(cell, 0, 768))
         tt(B("CM"), B("CT", 0, 768, 32), B("CT", 16, 768, 32), OP.max)
         cp(B("OFC"), B("CM"))

@@ -8,11 +8,11 @@ EARLY = 4
 LISTS = ("float8_e4m3fn_x4 QX 384 QU 128 UQ 1024 QV 128 WQ 512 QE 512 QM 256 QT 256 QB 128 LB 128",
          "uint8 SX 384 SU 128 US 1024 SV 128 WS 512 SE 512 SM 256 SQ 256 SB 128 LS 128",
          "bfloat16 X 1024 UIN 512 VIN 512 ONES 512 EB 2048 VP 1536 M 1024 TT 1024 DW 1088 CELL0 816 CELL1 816 "
-         "CELL2 816 POS 256 CT 768 UB 512",
-         "float32 IOTA 768 TAB 6144 SCP 3456 STB 36 SCN 512 CS 256 GT 64 GB 32 GA 32 ZB 32 BU 16 AB 16 FA 16 NB 16 UNW 256 "
-         "CEA 16 EE 512 DS 512 FLB 16 MXB 16 CM 24 FU 512 MASK 64 MINM 32 RM 64 CDG 512 PF 8 YO 256 ONR 256",
-         "int32 LST 384 NI 16 T1 16 MD 64 MDA 64 ME 512 MF 512 MI 64 MJ 64 PI 8 UOI 64 RI 32",
-         "uint16 LSU 384 OFG 32 OFW 32 NU 16 OFN 16 OFS 16 OFC 24 UOF 64 REP 32 REV 16")
+         "CELL2 816 CELL3 816 CELL4 816 CELL5 816 POS 256 CT0 768 CT1 768 UB 512",
+         "float32 IOTA 768 TAB 6144 SCP 3456 PQ 64 SCN 1024 CS 256 GT 128 GB 32 GA 32 D1 32 D2 32 BU 16 AB 16 FA 16 NB 16 "
+         "UNW 256 CEA 16 EE 512 DS 512 FLB 16 MXB 16 CM 24 CA 24 CB 24 FU 512 MASK 128 MINM 32 RM 128 CDG 512 PF 8 YO 256 ONR 256",
+         "int32 LST 384 NI 16 T1 16 MD 128 MDA 128 ME 512 MF 512 MI 128 MJ 128 PI 8 UOI 64 RI 32",
+         "uint16 LSU 384 OF 64 NU 16 OFN 16 OFS 16 OFC 24 UOF 64 REP 32 REV 16")
 WIDTH = {}
 SCRATCH = {}
 for _line in LISTS:
@@ -23,7 +23,7 @@ for _line in LISTS:
 for _i in range(8):
     WIDTH["ps%d" % _i] = 512
     SCRATCH["ps%d" % _i] = ("psum", [128, 512], "float32")
-SEMAPHORES = ["v", "s", "pe", "gp", "lx0", "lx1", "lu", "lv", "lwc", "lws", "la", "lb", "lr", "exa", "exb", "exc", "outs",
+SEMAPHORES = ["v", "s", "pe", "gp", "lx0", "lx1", "lu", "lv", "lwc", "lws", "la", "lb", "lr", "exa", "exb", "exc", "exd", "outs",
               "oute", "brd", "bar", "sbrd", "sbar"]
 
 
@@ -171,8 +171,8 @@ def rank_program(g, core, T, topo):
     iota(B("PI", 0, 1), 1, 0, 1)
     iota(B("IOTA", E, 2 * E), E, E, 0)
     fill(B("ONES"), 1.0)
-    cp(B("MI"), B("IOTA", 0, 64))
-    ts(B("UOI"), B("MI"), 0x38, OP.bitwise_and)
+    cp(B("MI"), B("IOTA", 0, 128))
+    ts(B("UOI"), B("MI", 0, 64), 0x38, OP.bitwise_and)
     ts(B("UOF"), B("UOI"), 2, OP.mult)
     cp(B("PF", 0, 1), B("PI", 0, 1))
     quant("QX", "SX", 0, H, "X")
@@ -189,19 +189,18 @@ def rank_program(g, core, T, topo):
     quant("QX", "SX", H, C, "X")
     for k in range(8):
         score(k, 0, C)
-    ts(B("MD"), B("IOTA", 0, 64), B("PF", 0, 1), OP.subtract, 256.0, OP.add)
+    ts(B("MD"), B("IOTA", 0, 128), B("PF", 0, 1), OP.subtract, 256.0, OP.add)
     ts(B("PI", 1, 2), B("PI", 0, 1), 7, OP.bitwise_and)
-    ts(B("MDA"), B("MD"), 15, OP.bitwise_and)
     ts(B("PI", 2, 3), B("PI", 0, 1), 3, OP.arith_shift_right)
-    ts(B("MASK"), B("MDA"), 0, OP.is_equal)
+    ts(B("MDA"), B("MD"), 15, OP.bitwise_and)
     ts(B("PF", 5, 6), B("PI", 1, 2), 32, OP.mult)
-    ts(B("MINM"), B("MASK", 0, 32), 1e29, OP.mult, -1.0, OP.add)
-    tt(B("PF", 1, 2), B("PF", 5, 6), B("PI", 2, 3), OP.add)
     ts(B("MJ"), B("MI"), 15, OP.bitwise_and)
-    for x in range(4):
-        ts(B("STB", x, x + 1), B("PF", 1, 2), -1.0, OP.mult, float(255 - 16 * (x % 2) + E * (x // 2)), OP.add)
+    ts(B("MASK"), B("MDA"), 0, OP.is_equal)
+    tt(B("PF", 1, 2), B("PF", 5, 6), B("PI", 2, 3), OP.add)
     ts(B("RM"), B("MJ"), 0, OP.not_equal)
-    cp(B("OFG", 0, 4), B("STB", 0, 4))
+    ts(B("MINM"), B("MASK", 0, 32), 1e29, OP.mult, -1.0, OP.add)
+    for x in range(4):
+        ts(B("OF", 2 + x, 3 + x), B("PF", 1, 2), -1.0, OP.mult, float(255 - 16 * (x % 2) + E * (1 - x // 2)), OP.add)
     cp(B("LSU"), B("LST"))
 
     def table(q, k):
@@ -212,31 +211,36 @@ def rank_program(g, core, T, topo):
     def col(buf, x):
         return B(buf, x, x + 1)
 
-    def gather_ends(k):
-        tt(B("GT"), B("TAB", 768 * k, 768 * k + 768, ix=B("OFG", 4 * k, 4 * k + 4)), B("MASK"), OP.mult)
-        spare()
-        scan(B("SCN", 64 * k, 64 * k + 64), B("RM"), B("GT"), OP.mult, OP.add)
-        spare()
-        cp(B("OFW", 4 * k, 4 * k + 4), B("SCN", 64 * k + 15, 64 * k + 64, 16))
-        spare()
+    def candidates(k):
+        tt(B("GT"), B("TAB", 768 * k + 768, 768 * k + 1536, ix=B("OF", 8 * k, 8 * k + 8)), B("MASK"), OP.mult)
 
-    def diff(k, x):
-        n = 4 * k + 2 * x
-        w, o = B("SCN", 64 * k + 15 + 32 * x, 64 * k + 32 + 32 * x, 16), B("STB", n, n + 2)
-        tt(B("ZB", n, n + 2), *((o, w) if x else (w, o)), OP.subtract)
+    def candidates_own(k):
+        scan(B("SCN", 128 * k, 128 * k + 128), B("RM"), B("GT"), OP.mult, OP.add)
+
+    def diff_ends(k):
+        tt(B("D2", 4 * k, 4 * k + 4), B("PQ", 8 * k, 8 * k + 4), B("PQ", 8 * k + 4, 8 * k + 8), OP.subtract)
+
+    def diff_candidates(k):
+        tt(B("D1", 4 * k, 4 * k + 4), B("SCN", 128 * k + 15, 128 * k + 64, 16), B("SCN", 128 * k + 79, 128 * k + 128, 16), OP.subtract)
 
     table("v", 0)
-    gather_ends(0)
-    diff(0, 0)
-    diff(0, 1)
+    tt(B("GT", 0, 64), B("TAB", 0, 768, ix=B("OF", 2, 6)), B("MASK", 0, 64), OP.mult)
+    scan(B("SCN", 0, 64), B("RM", 0, 64), B("GT", 0, 64), OP.mult, OP.add)
+    cp(B("OF", 6, 8), B("SCN", 15, 32, 16))
+    cp(B("OF", 0, 2), B("SCN", 47, 64, 16))
+    table("v", 1)
+    cp(B("PQ", 0, 8), B("OF", 0, 8))
+    candidates(0)
+    diff_ends(0)
+    candidates_own(0)
+    diff_candidates(0)
     later(ts, B("PI", 3, 4), B("PI", 0, 1), 15, OP.bitwise_and)
     later(ts, B("PI", 4, 5), B("PI", 0, 1), 16, OP.bitwise_and)
-    later(fill, B("CELL0"), 0.0)
+    later(quant, "QE", "SE", 0, 512, "EB")
     later(cp, B("PF", 4, 5), B("PI", 3, 4))
     later(cp, B("PF", 3, 4), B("PI", 4, 5))
     later(ts, B("PF", 2, 3), B("PI", 3, 4), 768, OP.add)
     later(ts, B("PF", 6, 7), B("PI", 3, 4), 784, OP.add)
-    later(quant, "QE", "SE", 0, 512, "EB")
     for x in range(2):
         later(ts, B("ME", 256 * x, 256 * x + 256), B("IOTA", 0, 256), B("PF", 4, 5), OP.subtract, 256.0 - 16 * x, OP.add)
         later(ts, B("RI", 16 * x, 16 * x + 16), B("MI", 0, 16), 14, OP.bitwise_and)
@@ -246,12 +250,12 @@ def rank_program(g, core, T, topo):
     later(ts, B("CDG"), B("MF"), 0, OP.not_equal)
     later(ts, B("PF", 7, 8), B("PF", 4, 5), -1.0, OP.mult, 255.0, OP.add)
     later(ts, B("POS"), B("IOTA", 0, 256), 1.0, OP.add)
+    later(fill, B("CELL0"), 0.0)
+    later(fill, B("CELL1"), 0.0)
     later(ts, B("REV"), B("IOTA", 0, 16), -16.0, OP.mult, B("PF", 7, 8), OP.add)
     for b in range(4):
         later(fill, B("DW", PW * b, PW * b + 1), 0.0)
     later(quant, "QV", "SV", 0, 128, "VIN")
-    for t in range(1, R):
-        later(fill, B("CELL%d" % t), 0.0)
 
     def list_out(k, sem):
         dma("y", sem, B("OFN", p=(16 * k, 16 * k + 16)), B("NU", 2 * k, 2 * k + 2))
@@ -266,14 +270,23 @@ def rank_program(g, core, T, topo):
                 list_out(k, sem)
 
         for j in range(2):
-            later(ts, part("BU", j), B("SCN", 64 * k0 + 47 + 16 * j, 64 * k1, 64), -float(E), OP.add, to=soon)
+            later(ts, part("BU", j), B("PQ", 8 * k0 + 6 + j, 8 * k1, 8), -float(E), OP.add, to=soon)
         for j in range(2):
-            later(tt, part("AB", j), B("SCN", 64 * k0 + 15 + 16 * j, 64 * k1, 64), part("BU", j), OP.subtract, to=soon)
+            later(tt, part("AB", j), B("PQ", 8 * k0 + j, 8 * k1, 8), part("BU", j), OP.subtract, to=soon)
         for j in range(2):
             later(tt, part("FA", j), B("CS", 32 * k0 + 15 + 16 * j, 32 * k1, 32), part("AB", j), OP.mult, to=soon)
         for j in range(2):
             later(tt, part("NB", j), part("FA", j), part("BU", j), OP.add, to=soon)
         later(end, to=soon)
+
+    def right_place(k):
+        ts(B("BU", 2 * k, 2 * k + 2), B("PQ", 8 * k + 6, 8 * k + 8), -float(E), OP.add)
+
+    def place_diff(k):
+        tt(B("AB", 2 * k, 2 * k + 2), B("PQ", 8 * k, 8 * k + 2), B("BU", 2 * k, 2 * k + 2), OP.subtract)
+
+    def place(k, j):
+        ts(col("NU", 2 * k + j), col("CS", 32 * k + 15 + 16 * j), col("AB", 2 * k + j), OP.mult, col("BU", 2 * k + j), OP.add)
 
     for t in range(R):
         last = t == R - 1
@@ -283,47 +296,61 @@ def rank_program(g, core, T, topo):
                 act(B("VP", E * b, E * b + E), mm("QE", "SE", 128 * b, "QX", "SX", 0, E))
 
         if t == 0:
-            table("s", 1)
+            table("s", 2)
         for k in range(8):
             score(k, C, E)
-            if t == 0 and 1 <= k < 7:
-                table("s", k + 1)
+            if t == 0 and 1 <= k < 6:
+                table("s", k + 2)
         if t:
             numbers()
         for k in range(8):
-            if t == 0 and k == 5:
+            if t == 0 and k == 3:
                 numbers()
-            if k:
-                gather_ends(k)
-            o, f, c, n = E * k, 64 * k, 32 * k, 4 * k + 4
-            tt(B("GB"), B("SCP", o, o + 2 * E, ix=B("OFW", 4 * k + 2, 4 * k + 4)), B("MINM"), OP.min)
+            o, c, n = E * k, 32 * k, 8 * k
+            tt(B("GB"), B("SCP", o, o + 2 * E, ix=B("OF", n + 6, n + 8)), B("MINM"), OP.min)
             if 0 < k < 7:
-                diff(k, 0)
-            if k == 7:
-                ts(B("BU", 14, 16), B("SCN", f + 47, f + 64, 16), -float(E), OP.add)
-            tt(B("GA"), B("SCP", o + E, o + 2 * E, ix=B("OFW", 4 * k, 4 * k + 2)), B("GB"), OP.is_le)
+                candidates(k)
+                cp(B("PQ", n, n + 8), B("OF", n, n + 8))
+            elif k == 7:
+                cp(B("PQ", n + 6, n + 8), B("OF", n + 6, n + 8))
+                cp(B("PQ", n, n + 2), B("OF", n, n + 2))
+            else:
+                spare()
+            tt(B("GA"), B("SCP", o + E, o + 2 * E, ix=B("OF", n, n + 2)), B("GB"), OP.is_le)
             if 0 < k < 7:
-                diff(k, 1)
-            if k == 7:
-                tt(B("AB", 14, 16), B("SCN", f + 15, f + 32, 16), B("BU", 14, 16), OP.subtract)
+                candidates_own(k)
+            elif k == 7:
+                right_place(k)
+                spare()
+            if 0 < k < 6:
+                diff_ends(k)
             spare()
             scan(B("CS", c, c + 32), B("RM", 0, 32), B("GA"), OP.mult, OP.add)
-            spare()
+            if 0 < k < 7:
+                diff_candidates(k)
+            elif k == 7:
+                place_diff(k)
             if k < 7:
-                for x in range(4):
-                    base = col("SCN", f + 15 + 16 * x) if x > 1 else col("STB", 4 * k + x)
-                    ts(col("OFG", n + x), col("CS", c + 15 + 16 * (x % 2)), col("ZB", 4 * k + x), OP.mult, base, OP.add)
-                soon.insert(0, lambda n=n: cp(B("STB", n, n + 4), B("OFG", n, n + 4)))
+                for x in range(4 if k < 6 else 0):
+                    ts(col("OF", n + 8 + (4 + x if x < 2 else x)), col("CS", c + 15 + 16 * (x % 2)), col("D2", 4 * k + x), OP.mult, col("PQ", n + 4 + x), OP.add)
+                spare()
+                for x in (2, 3, 0, 1):
+                    ts(col("OF", n + 8 + (4 + x if x > 1 else x)), col("CS", c + 15 + 16 * (x % 2)), col("D1", 4 * k + x), OP.mult,
+                       col("SCN", 128 * k + 79 + 16 * x), OP.add)
+                if k >= 5:
+                    later(right_place, k, to=soon)
+                    later(place_diff, k, to=soon)
+                    later(place, k, 0, to=soon)
+                    later(place, k, 1, to=soon)
+                    later(list_out, k, "exb" if k == 5 else "exc", to=soon)
+                elif k == 4:
+                    lists_out(0, 5, "exa")
             else:
                 while soon:
                     spare()
                 for j in range(2):
-                    ts(col("NU", 14 + j), col("CS", c + 15 + 16 * j), col("AB", 14 + j), OP.mult, col("BU", 14 + j), OP.add)
-                list_out(7, "exc")
-            if k == 3:
-                lists_out(0, 4, "exa")
-            if k == 6:
-                lists_out(4, 7, "exb")
+                    place(k, j)
+                list_out(k, "exd")
         for b in (0, 2, 1, 3):
             (cp if b < 2 else act)(B("M", b, 1024, 4), B("VP", E * b, E * b + E, ix=B("OFN")))
         quant("QM", "SM", 0, C, "M")
@@ -345,11 +372,14 @@ def rank_program(g, core, T, topo):
         quant("QT", "SQ", 0, C, "TT")
         for b in range(4):
             act(B("DW", PW * b + 1, PW * b + 257), mm("QE", "SE", 128 * b, "QT", "SQ", 0, C), scale=-1.0)
-        cell = "CELL%d" % t
+        cell = ("CELL%d" % (2 * t), "CELL%d" % (2 * t + 1))
         for w in range(8):
-            cp(B(cell, ix=B("OFS", 2 * w, 2 * w + 2)), B("POS", 32 * w, 32 * w + 32))
-        run("v", v.transpose, B("CT"), B(cell, 0, 768))
-        tt(B("CM"), B("CT", 0, 768, 32), B("CT", 16, 768, 32), OP.max)
+            cp(B(cell[w % 2], ix=B("OFS", 2 * w, 2 * w + 2)), B("POS", 32 * w, 32 * w + 32))
+        for x in range(2):
+            run("v", v.transpose, B("CT%d" % x), B(cell[x], 0, 768))
+        for x in range(2):
+            tt(B("CB" if x else "CA"), B("CT%d" % x, 0, 768, 32), B("CT%d" % x, 16, 768, 32), OP.max)
+        tt(B("CM"), B("CA"), B("CB"), OP.max)
         cp(B("OFC"), B("CM"))
 
         def taken(b, w0, w1):
@@ -381,6 +411,8 @@ def rank_program(g, core, T, topo):
             dma("y", "outs", T.on[:], (T.ONR[0:128:16, :], B("ONR")[1]))
             result(H, C)
         else:
+            fill(B("CELL%d" % (2 * t + 2)), 0.0)
+            fill(B("CELL%d" % (2 * t + 3)), 0.0)
             for k in range(EARLY):
                 score(k, H, C)
         for b in range(4):

@@ -3,8 +3,10 @@ from concourse.mybir import dt, AluOpType, ActivationFunctionType
 OP = AluOpType
 AF = ActivationFunctionType
 N, R, C, H, E = 8, 3, 256, 128, 384
+CW = 816
 PW = 272
 EARLY = 4
+PRE = 2
 LISTS = ("float8_e4m3fn_x4 QX 384 QU 128 UQ 1024 QV 128 WQ 512 QE 512 QM 256 QT 256 QB 128 LB 128",
          "uint8 SX 384 SU 128 US 1024 SV 128 WS 512 SE 512 SM 256 SQ 256 SB 128 LS 128",
          "bfloat16 X 1024 UIN 512 VIN 512 ONES 512 EB 2048 VP 1536 M 1024 TT 1024 DW 1088 CELL0 816 CELL1 816 "
@@ -23,8 +25,8 @@ for _line in LISTS:
 for _i in range(8):
     WIDTH["ps%d" % _i] = 512
     SCRATCH["ps%d" % _i] = ("psum", [128, 512], "float32")
-SEMAPHORES = ["v", "s", "pe", "gp", "lx0", "lx1", "lu", "lv", "lwc", "lws", "la", "lb", "lr", "exa", "exb", "exc", "exd", "outs",
-              "oute", "brd", "bar", "sbrd", "sbar"]
+SEMAPHORES = ["v", "s", "pe", "gp", "lx0", "lx1", "lu", "lv", "lwc", "lws", "la", "lb", "lr", "exa", "ex4", "ex5", "ex6",
+              "ex7", "outs", "oute", "brd", "bar", "sbrd", "sbar"]
 
 
 def rank_program(g, core, T, topo):
@@ -129,8 +131,8 @@ def rank_program(g, core, T, topo):
     def fill(x, c):
         run("v", v.memset, x, c)
 
-    def iota(out, n, base, cm):
-        run("g", g.iota, out, [[1, n]], base, cm, allow_small_or_imprecise_dtypes=True)
+    def iota(out, step, n, base, cm):
+        run("g", g.iota, out, [[step, n]], base, cm, allow_small_or_imprecise_dtypes=True)
 
     def quant(q, sc, a, b, tile):
         run("v", v.quantize_mx, B(q, a, b), B(sc, a, b), B(tile, 4 * a, 4 * b), outs=2)
@@ -153,8 +155,8 @@ def rank_program(g, core, T, topo):
     soon, todo = [], []
 
     def spare():
-        if soon or todo:
-            (soon or todo).pop(0)()
+        if soon:
+            soon.pop(0)()
 
     def later(f, *a, to=todo):
         to.append(lambda: f(*a))
@@ -167,9 +169,9 @@ def rank_program(g, core, T, topo):
     dma("y", "lx1", B("X", 512, 1024), T.x[:, 512:1024])
     for h in range(1, 8):
         dma("y", "lr", B("LST", p=(16 * h, 16 * h + 16)), B("LST", p=(0, 16)))
-    iota(B("IOTA", 0, E), E, 0, 0)
-    iota(B("PI", 0, 1), 1, 0, 1)
-    iota(B("IOTA", E, 2 * E), E, E, 0)
+    iota(B("IOTA", 0, E), 1, E, 0, 0)
+    iota(B("PI", 0, 1), 1, 1, 0, 1)
+    iota(B("IOTA", E, 2 * E), 1, E, E, 0)
     fill(B("ONES"), 1.0)
     cp(B("MI"), B("IOTA", 0, 128))
     ts(B("UOI"), B("MI", 0, 64), 0x38, OP.bitwise_and)
@@ -177,9 +179,12 @@ def rank_program(g, core, T, topo):
     cp(B("PF", 0, 1), B("PI", 0, 1))
     quant("QX", "SX", 0, H, "X")
     send_border()
-    iota(B("SCP", 0, E), E, 0, 0)
+    iota(B("SCP", 0, E), 1, E, 0, 0)
     for b in range(4):
         run("g", g.affine_select, B("EB", 512 * b, 512 * b + 512), B("ONES"), [[-8, 128], [-1, 4]], OP.is_equal, 0.0, b, 8)
+    iota(B("POS"), 1, 256, 1, 0)
+    for x in range(2 * R):
+        iota(B("CELL%d" % x), 0, CW, 0, 0)
     dma("s", "lwc", B("WQ", bit=dt.uint8), T.wc[:])
     dma("s", "lws", B("WS"), T.ws[:])
     dma("y", "lv", B("VIN"), T.v[:])
@@ -236,26 +241,22 @@ def rank_program(g, core, T, topo):
     diff_candidates(0)
     later(ts, B("PI", 3, 4), B("PI", 0, 1), 15, OP.bitwise_and)
     later(ts, B("PI", 4, 5), B("PI", 0, 1), 16, OP.bitwise_and)
-    later(quant, "QE", "SE", 0, 512, "EB")
+    for x in range(2):
+        later(ts, B("RI", 16 * x, 16 * x + 16), B("MI", 0, 16), 14, OP.bitwise_and)
     later(cp, B("PF", 4, 5), B("PI", 3, 4))
     later(cp, B("PF", 3, 4), B("PI", 4, 5))
     later(ts, B("PF", 2, 3), B("PI", 3, 4), 768, OP.add)
     later(ts, B("PF", 6, 7), B("PI", 3, 4), 784, OP.add)
     for x in range(2):
         later(ts, B("ME", 256 * x, 256 * x + 256), B("IOTA", 0, 256), B("PF", 4, 5), OP.subtract, 256.0 - 16 * x, OP.add)
-        later(ts, B("RI", 16 * x, 16 * x + 16), B("MI", 0, 16), 14, OP.bitwise_and)
-    later(ts, B("MF"), B("ME"), 31, OP.bitwise_and)
-    for x in range(2):
         later(ts, B("REP", 16 * x, 16 * x + 16), B("RI", 16 * x, 16 * x + 16), x, OP.add)
-    later(ts, B("CDG"), B("MF"), 0, OP.not_equal)
     later(ts, B("PF", 7, 8), B("PF", 4, 5), -1.0, OP.mult, 255.0, OP.add)
-    later(ts, B("POS"), B("IOTA", 0, 256), 1.0, OP.add)
-    later(fill, B("CELL0"), 0.0)
-    later(fill, B("CELL1"), 0.0)
-    later(ts, B("REV"), B("IOTA", 0, 16), -16.0, OP.mult, B("PF", 7, 8), OP.add)
+    later(ts, B("MF"), B("ME"), 31, OP.bitwise_and)
+    later(quant, "QV", "SV", 0, 128, "VIN")
     for b in range(4):
         later(fill, B("DW", PW * b, PW * b + 1), 0.0)
-    later(quant, "QV", "SV", 0, 128, "VIN")
+    later(ts, B("CDG"), B("MF"), 0, OP.not_equal)
+    later(ts, B("REV"), B("IOTA", 0, 16), -16.0, OP.mult, B("PF", 7, 8), OP.add)
 
     def list_out(k, sem):
         dma("y", sem, B("OFN", p=(16 * k, 16 * k + 16)), B("NU", 2 * k, 2 * k + 2))
@@ -285,8 +286,10 @@ def rank_program(g, core, T, topo):
     def place_diff(k):
         tt(B("AB", 2 * k, 2 * k + 2), B("PQ", 8 * k, 8 * k + 2), B("BU", 2 * k, 2 * k + 2), OP.subtract)
 
-    def place(k, j):
-        ts(col("NU", 2 * k + j), col("CS", 32 * k + 15 + 16 * j), col("AB", 2 * k + j), OP.mult, col("BU", 2 * k + j), OP.add)
+    def places(k):
+        for j in range(2):
+            ts(col("NU", 2 * k + j), col("CS", 32 * k + 15 + 16 * j), col("AB", 2 * k + j), OP.mult, col("BU", 2 * k + j), OP.add)
+        list_out(k, "ex%d" % k)
 
     for t in range(R):
         last = t == R - 1
@@ -305,6 +308,7 @@ def rank_program(g, core, T, topo):
             numbers()
         for k in range(8):
             if t == 0 and k == 3:
+                quant("QE", "SE", 0, 512, "EB")
                 numbers()
             o, c, n = E * k, 32 * k, 8 * k
             tt(B("GB"), B("SCP", o, o + 2 * E, ix=B("OF", n + 6, n + 8)), B("MINM"), OP.min)
@@ -314,21 +318,19 @@ def rank_program(g, core, T, topo):
             elif k == 7:
                 cp(B("PQ", n + 6, n + 8), B("OF", n + 6, n + 8))
                 cp(B("PQ", n, n + 2), B("OF", n, n + 2))
-            else:
                 spare()
             tt(B("GA"), B("SCP", o + E, o + 2 * E, ix=B("OF", n, n + 2)), B("GB"), OP.is_le)
             if 0 < k < 7:
                 candidates_own(k)
-            elif k == 7:
-                right_place(k)
-                spare()
             if 0 < k < 6:
                 diff_ends(k)
+            if k > 3:
+                right_place(k)
             spare()
             scan(B("CS", c, c + 32), B("RM", 0, 32), B("GA"), OP.mult, OP.add)
             if 0 < k < 7:
                 diff_candidates(k)
-            elif k == 7:
+            if k > 3:
                 place_diff(k)
             if k < 7:
                 for x in range(4 if k < 6 else 0):
@@ -337,44 +339,53 @@ def rank_program(g, core, T, topo):
                 for x in (2, 3, 0, 1):
                     ts(col("OF", n + 8 + (4 + x if x > 1 else x)), col("CS", c + 15 + 16 * (x % 2)), col("D1", 4 * k + x), OP.mult,
                        col("SCN", 128 * k + 79 + 16 * x), OP.add)
-                if k >= 5:
-                    later(right_place, k, to=soon)
-                    later(place_diff, k, to=soon)
-                    later(place, k, 0, to=soon)
-                    later(place, k, 1, to=soon)
-                    later(list_out, k, "exb" if k == 5 else "exc", to=soon)
-                elif k == 4:
-                    lists_out(0, 5, "exa")
+                if k > 3:
+                    places(k)
+                elif k == 3:
+                    lists_out(0, 4, "exa")
             else:
                 while soon:
                     spare()
-                for j in range(2):
-                    place(k, j)
-                list_out(k, "exd")
-        for b in (0, 2, 1, 3):
-            (cp if b < 2 else act)(B("M", b, 1024, 4), B("VP", E * b, E * b + E, ix=B("OFN")))
-        quant("QM", "SM", 0, C, "M")
+                places(k)
         while todo:
-            spare()
+            todo.pop(0)()
+
+        def flux(f, b):
+            f(B("M", b, 1024, 4), B("VP", E * b, E * b + E, ix=B("OFN")))
+
         act(B("UNW"), B("IOTA", 0, E, ix=B("OFN")))
+        for b in range(2):
+            flux(cp, b)
+            flux(act, b + 2)
+        def equal(x):
+            tt(B("EE", 256 * x, 256 * x + 256), B("NI", ix=B("REP", 16 * x, 16 * x + 16)), B("UNW"), OP.is_equal)
+
         cp(B("NI"), B("OFN"))
         ts(B("T1"), B("NI"), 0x1F0, OP.bitwise_and)
-        for x in range(2):
-            tt(B("EE", 256 * x, 256 * x + 256), B("NI", ix=B("REP", 16 * x, 16 * x + 16)), B("UNW"), OP.is_equal)
+        equal(0)
+        quant("QM", "SM", 0, C, "M")
+        equal(1)
         tt(B("CEA"), B("NI"), B("T1"), OP.add)
-        scan(B("DS"), B("EE"), B("CDG"), OP.max, OP.mult)
+        for x in range(2):
+            scan(B("DS", 256 * x, 256 * x + 256), B("EE", 256 * x, 256 * x + 256), B("CDG", 256 * x, 256 * x + 256), OP.max, OP.mult)
         for x in range(2):
             ts(B("FLB", x, 16, 2), B("DS", 256 * x + 31, 256 * x + 256, 32), B("PF", 6, 7) if x else B("PF", 2, 3), OP.mult)
         tt(B("MXB"), B("CEA"), B("FLB"), OP.max)
         ts(B("OFS"), B("MXB"), B("PF", 3, 4), OP.add)
+        cell = ("CELL%d" % (2 * t), "CELL%d" % (2 * t + 1))
+
+        def scatter(w):
+            cp(B(cell[w % 2], ix=B("OFS", 2 * w, 2 * w + 2)), B("POS", 32 * w, 32 * w + 32))
+
+        for w in range(PRE):
+            scatter(w)
         for b in range(4):
             act(B("TT", b, 1024, 4), mm("WQ", "WS", 128 * b, "QM", "SM", 0, C), scale=0.03125)
         quant("QT", "SQ", 0, C, "TT")
         for b in range(4):
             act(B("DW", PW * b + 1, PW * b + 257), mm("QE", "SE", 128 * b, "QT", "SQ", 0, C), scale=-1.0)
-        cell = ("CELL%d" % (2 * t), "CELL%d" % (2 * t + 1))
-        for w in range(8):
-            cp(B(cell[w % 2], ix=B("OFS", 2 * w, 2 * w + 2)), B("POS", 32 * w, 32 * w + 32))
+        for w in range(PRE, 8):
+            scatter(w)
         for x in range(2):
             run("v", v.transpose, B("CT%d" % x), B(cell[x], 0, 768))
         for x in range(2):
@@ -411,8 +422,6 @@ def rank_program(g, core, T, topo):
             dma("y", "outs", T.on[:], (T.ONR[0:128:16, :], B("ONR")[1]))
             result(H, C)
         else:
-            fill(B("CELL%d" % (2 * t + 2)), 0.0)
-            fill(B("CELL%d" % (2 * t + 3)), 0.0)
             for k in range(EARLY):
                 score(k, H, C)
         for b in range(4):

from concourse.mybir import dt, AluOpType, ActivationFunctionType

OP = AluOpType
AF = ActivationFunctionType
N, R, C, H, E = 8, 3, 256, 128, 384
CW = 816
PW = 272
EARLY = 4
PRE = 2
LISTS = ("float8_e4m3fn_x4 QX 384 QU 128 UQ 1024 QV 128 WQ 512 QE 512 QM 256 QT 256 QB 128 LB 128",
         "uint8 SX 384 SU 128 US 1024 SV 128 WS 512 SE 512 SM 256 SQ 256 SB 128 LS 128",
         "bfloat16 X 1024 UIN 512 VIN 512 ONES 512 EB 2048 VP 1536 M 1024 TT 1024 DW 1088 CELL0 816 CELL1 816 "
         "CELL2 816 CELL3 816 CELL4 816 CELL5 816 POS 256 CT0 768 CT1 768 UB 512",
         "float32 IOTA 768 TAB 6144 SCP 3456 PQ 64 SCN 1024 CS 256 GT 128 GB 32 GA 32 D1 32 D2 32 BU 16 AB 16 FA 16 NB 16 "
         "UNW 256 CEA 16 EE 512 DS 512 FLB 16 MXB 16 CM 24 CA 24 CB 24 FU 512 MASK 128 MINM 32 RM 128 CDG 512 PF 8 YO 256 ONR 256",
         "int32 LST 384 NI 16 T1 16 MD 128 MDA 128 ME 512 MF 512 MI 128 MJ 128 PI 8 UOI 64 RI 32",
         "uint16 LSU 384 OF 64 NU 16 OFN 16 OFS 16 OFC 24 UOF 64 REP 32 REV 16")
WIDTH = {}
SCRATCH = {}
for _line in LISTS:
    _w = _line.split()
    for _i in range(1, len(_w), 2):
        WIDTH[_w[_i]] = int(_w[_i + 1])
        SCRATCH[_w[_i]] = ("sbuf", [128, int(_w[_i + 1])], _w[0])
for _i in range(8):
    WIDTH["ps%d" % _i] = 512
    SCRATCH["ps%d" % _i] = ("psum", [128, 512], "float32")
SEMAPHORES = ["v", "s", "pe", "gp", "lx0", "lx1", "lu", "lv", "lwc", "lws", "la", "lb", "lr", "exa", "ex4", "ex5", "ex6",
              "ex7", "outs", "oute", "brd", "bar", "sbrd", "sbar"]


def rank_program(g, core, T, topo):
    rank = T.rank_of(core)
    if rank is None:
        return
    nxt, prv = T.cores[(rank + 1) % N], T.cores[(rank - 1) % N]
    v, s = g.vector, g.scalar
    eng = {"pe": g.tensor, "v": v, "s": s, "g": g, "y": g.sync}
    home = {"pe": "pe", "v": "v", "s": "s", "g": "gp"}
    count = {k: 0 for k in SEMAPHORES}
    held = {}
    log = {}

    def B(n, a=0, b=None, st=1, ix=None, bit=None, p=(0, 128)):
        b = WIDTH[n] if b is None else b
        ap = T[n][p[0]:p[1], a:b] if st == 1 else T[n][p[0]:p[1], a:b:st]
        if bit:
            ap = ap.bitcast(bit)
        if ix:
            ap = ap.indirect(ix[0])
        return (ap, [(n, p[0], p[1], a, b, st)], ix[1] if ix else [])

    def wait(q, sem, val):
        if held.get((q, sem), 0) < val:
            held[(q, sem)] = val
            eng[q].wait_ge(T.sem[sem], val)

    def order(q, reads, writes):
        need = {}
        for kinds, regs in (("wW", reads), ("rw", writes)):
            for n, p0, p1, c0, c1, st in regs:
                for k, a0, a1, b0, b1, su, sem, val, far in log.get(n, ()):
                    if k in kinds and a0 < p1 and p0 < a1 and b0 < c1 and c0 < b1 and (st != su or (c0 - b0) % st == 0):
                        need[sem] = max(need.get(sem, 0), count[sem] if far else val)
        for sem in need:
            wait(q, sem, need[sem])

    def note(reads, writes, sem, far):
        for n, p0, p1, c0, c1, st in writes:
            log[n] = [x for x in log.get(n, ()) if not (p0 <= x[1] and x[2] <= p1 and c0 <= x[3] and x[4] <= c1
                                                        and (st == 1 or st == x[5] and (c0 - x[3]) % st == 0))]
        for n, p0, p1, c0, c1, st in reads:
            if st == 1:
                log[n] = [("W",) + x[1:] if x[0] == "w" and p0 <= x[1] and x[2] <= p1 and c0 <= x[3] and x[4] <= c1 else x
                          for x in log.get(n, ())]
        for kind, regs in (("w", writes), ("r", reads)):
            for r in regs:
                log.setdefault(r[0], []).append((kind,) + r[1:] + (sem, count[sem], far))

    def run(q, call, *args, outs=1, **kw):
        reads, writes, real = [], [], []
        for i, x in enumerate(args):
            if isinstance(x, tuple):
                (writes if i < outs else reads).extend(x[1])
                reads.extend(x[2])
                x = x[0]
            real.append(x)
        order(q, reads, writes)
        call(*real, **kw).then_inc(T.sem[home[q]], 1)
        count[home[q]] += 1
        note(reads, writes, home[q], False)

    def dma(q, sem, out, in_):
        w, r = (out[1] if isinstance(out, tuple) else []), (in_[1] if isinstance(in_, tuple) else [])
        order(q, r, w)
        eng[q].dma_start(out[0] if isinstance(out, tuple) else out, in_[0] if isinstance(in_, tuple) else in_).then_inc(T.sem[sem], 16)
        count[sem] += 16
        note(r, w, sem, True)

    def engines(a, b):
        return topo.engines(a, b)[:8]

    def exchange(dst, src, pairs, remote, local):
        reads = [r for o, i in pairs for r in i[1]]
        order("g", reads, [])
        rid, pid, _ = topo.addr(dst)
        es = engines(core, dst)
        for o, i in pairs:
            g.remote_dma(out_ap=o[0], in_ap=i[0], remote_sem=T.sem[remote], local_sem=T.sem[local], pid=pid, routing_id=rid,
                         dma_engine_mask=sum(1 << e for e in es))
            count[local] += len(es)
        note(reads, [], local, True)
        count[remote] += len(pairs) * len(engines(src, core))
        note([], [r for o, i in pairs for r in o[1]], remote, True)

    def ts(out, in0, s1, op0, s2=None, op1=None):
        run("v", v.tensor_scalar, out, in0, s1, s2, op0, *((op1,) if op1 else ()))

    def tt(out, in0, in1, op):
        run("v", v.tensor_tensor, out, in0, in1, op)

    def cp(out, in_):
        run("v", v.tensor_copy, out, in_)

    def act(out, in_, func=AF.Copy, **kw):
        run("s", s.activation, out, in_, func, **kw)

    def scan(out, d0, d1, op0, op1):
        run("v", v.tensor_tensor_scan, out, d0, d1, 0.0, op0, op1)

    def fill(x, c):
        run("v", v.memset, x, c)

    def iota(out, step, n, base, cm):
        run("g", g.iota, out, [[step, n]], base, cm, allow_small_or_imprecise_dtypes=True)

    def quant(q, sc, a, b, tile):
        run("v", v.quantize_mx, B(q, a, b), B(sc, a, b), B(tile, 4 * a, 4 * b), outs=2)

    bank = [0]

    def mm(lq, ls, la, rq, rs, a, b):
        p = "ps%d" % (bank[0] % 8)
        bank[0] += 1
        run("pe", g.tensor.matmul_mx, B(p, 0, b - a), B(lq, la, la + 128), B(ls, la, la + 128), B(rq, a, b), B(rs, a, b), True, True)
        return B(p, 0, b - a)

    def score(k, a, b):
        o = E * (k + 1)
        act(B("SCP", o + a, o + b), mm("UQ", "US", 128 * k, "QX", "SX", a, b), AF.Abs)

    def send_border():
        exchange(prv, nxt, ((B("QX", C, E, bit=dt.uint8), B("QX", 0, H, bit=dt.uint8)), (B("SX", C, E), B("SX", 0, H))), "brd", "sbrd")

    soon, todo = [], []

    def spare():
        if soon:
            soon.pop(0)()

    def later(f, *a, to=todo):
        to.append(lambda: f(*a))

    dma("y", "lx0", B("X", 0, 512), T.x[:, 0:512])
    dma("s", "lu", B("UIN"), T.u[:])
    for k in range(8):
        dma("y", "la", B("LST", 48 * k, 48 * k + 24, p=(0, 16)), T.lf[16 * k:16 * k + 16, :])
        dma("s", "lb", B("LST", 48 * k + 24, 48 * k + 48, p=(0, 16)), T.rt[16 * k:16 * k + 16, :])
    dma("y", "lx1", B("X", 512, 1024), T.x[:, 512:1024])
    for h in range(1, 8):
        dma("y", "lr", B("LST", p=(16 * h, 16 * h + 16)), B("LST", p=(0, 16)))
    iota(B("IOTA", 0, E), 1, E, 0, 0)
    iota(B("PI", 0, 1), 1, 1, 0, 1)
    iota(B("IOTA", E, 2 * E), 1, E, E, 0)
    fill(B("ONES"), 1.0)
    cp(B("MI"), B("IOTA", 0, 128))
    ts(B("UOI"), B("MI", 0, 64), 0x38, OP.bitwise_and)
    ts(B("UOF"), B("UOI"), 2, OP.mult)
    cp(B("PF", 0, 1), B("PI", 0, 1))
    quant("QX", "SX", 0, H, "X")
    send_border()
    iota(B("SCP", 0, E), 1, E, 0, 0)
    for b in range(4):
        run("g", g.affine_select, B("EB", 512 * b, 512 * b + 512), B("ONES"), [[-8, 128], [-1, 4]], OP.is_equal, 0.0, b, 8)
    iota(B("POS"), 1, 256, 1, 0)
    for x in range(2 * R):
        iota(B("CELL%d" % x), 0, CW, 0, 0)
    dma("s", "lwc", B("WQ", bit=dt.uint8), T.wc[:])
    dma("s", "lws", B("WS"), T.ws[:])
    dma("y", "lv", B("VIN"), T.v[:])
    quant("QU", "SU", 0, 128, "UIN")
    cp(B("UQ", bit=dt.uint32), B("QU", bit=dt.uint32, ix=B("UOF")))
    act(B("US"), B("SU", ix=B("UOF")))
    quant("QX", "SX", H, C, "X")
    for k in range(8):
        score(k, 0, C)
    ts(B("MD"), B("IOTA", 0, 128), B("PF", 0, 1), OP.subtract, 256.0, OP.add)
    ts(B("PI", 1, 2), B("PI", 0, 1), 7, OP.bitwise_and)
    ts(B("PI", 2, 3), B("PI", 0, 1), 3, OP.arith_shift_right)
    ts(B("MDA"), B("MD"), 15, OP.bitwise_and)
    ts(B("PF", 5, 6), B("PI", 1, 2), 32, OP.mult)
    ts(B("MJ"), B("MI"), 15, OP.bitwise_and)
    ts(B("MASK"), B("MDA"), 0, OP.is_equal)
    tt(B("PF", 1, 2), B("PF", 5, 6), B("PI", 2, 3), OP.add)
    ts(B("RM"), B("MJ"), 0, OP.not_equal)
    ts(B("MINM"), B("MASK", 0, 32), 1e29, OP.mult, -1.0, OP.add)
    for x in range(4):
        ts(B("OF", 2 + x, 3 + x), B("PF", 1, 2), -1.0, OP.mult, float(255 - 16 * (x % 2) + E * (1 - x // 2)), OP.add)
    cp(B("LSU"), B("LST"))

    def table(q, k):
        for x in range(2):
            o, l = 768 * k + E * x, 48 * k + 24 * x
            (cp if q == "v" else act)(B("TAB", o, o + E), B("IOTA", E * x, E * x + E, ix=B("LSU", l, l + 24)))

    def col(buf, x):
        return B(buf, x, x + 1)

    def candidates(k):
        tt(B("GT"), B("TAB", 768 * k + 768, 768 * k + 1536, ix=B("OF", 8 * k, 8 * k + 8)), B("MASK"), OP.mult)

    def candidates_own(k):
        scan(B("SCN", 128 * k, 128 * k + 128), B("RM"), B("GT"), OP.mult, OP.add)

    def diff_ends(k):
        tt(B("D2", 4 * k, 4 * k + 4), B("PQ", 8 * k, 8 * k + 4), B("PQ", 8 * k + 4, 8 * k + 8), OP.subtract)

    def diff_candidates(k):
        tt(B("D1", 4 * k, 4 * k + 4), B("SCN", 128 * k + 15, 128 * k + 64, 16), B("SCN", 128 * k + 79, 128 * k + 128, 16), OP.subtract)

    table("v", 0)
    tt(B("GT", 0, 64), B("TAB", 0, 768, ix=B("OF", 2, 6)), B("MASK", 0, 64), OP.mult)
    scan(B("SCN", 0, 64), B("RM", 0, 64), B("GT", 0, 64), OP.mult, OP.add)
    cp(B("OF", 6, 8), B("SCN", 15, 32, 16))
    cp(B("OF", 0, 2), B("SCN", 47, 64, 16))
    table("v", 1)
    cp(B("PQ", 0, 8), B("OF", 0, 8))
    candidates(0)
    diff_ends(0)
    candidates_own(0)
    diff_candidates(0)
    later(ts, B("PI", 3, 4), B("PI", 0, 1), 15, OP.bitwise_and)
    later(ts, B("PI", 4, 5), B("PI", 0, 1), 16, OP.bitwise_and)
    for x in range(2):
        later(ts, B("RI", 16 * x, 16 * x + 16), B("MI", 0, 16), 14, OP.bitwise_and)
    later(cp, B("PF", 4, 5), B("PI", 3, 4))
    later(cp, B("PF", 3, 4), B("PI", 4, 5))
    later(ts, B("PF", 2, 3), B("PI", 3, 4), 768, OP.add)
    later(ts, B("PF", 6, 7), B("PI", 3, 4), 784, OP.add)
    for x in range(2):
        later(ts, B("ME", 256 * x, 256 * x + 256), B("IOTA", 0, 256), B("PF", 4, 5), OP.subtract, 256.0 - 16 * x, OP.add)
        later(ts, B("REP", 16 * x, 16 * x + 16), B("RI", 16 * x, 16 * x + 16), x, OP.add)
    later(ts, B("PF", 7, 8), B("PF", 4, 5), -1.0, OP.mult, 255.0, OP.add)
    later(ts, B("MF"), B("ME"), 31, OP.bitwise_and)
    later(quant, "QV", "SV", 0, 128, "VIN")
    for b in range(4):
        later(fill, B("DW", PW * b, PW * b + 1), 0.0)
    later(ts, B("CDG"), B("MF"), 0, OP.not_equal)
    later(ts, B("REV"), B("IOTA", 0, 16), -16.0, OP.mult, B("PF", 7, 8), OP.add)

    def list_out(k, sem):
        dma("y", sem, B("OFN", p=(16 * k, 16 * k + 16)), B("NU", 2 * k, 2 * k + 2))

    def lists_out(k0, k1, sem):
        def part(buf, j):
            return B(buf, 2 * k0 + j, 2 * k1, 2)

        def end():
            cp(B("NU", 2 * k0, 2 * k1), B("NB", 2 * k0, 2 * k1))
            for k in range(k0, k1):
                list_out(k, sem)

        for j in range(2):
            later(ts, part("BU", j), B("PQ", 8 * k0 + 6 + j, 8 * k1, 8), -float(E), OP.add, to=soon)
        for j in range(2):
            later(tt, part("AB", j), B("PQ", 8 * k0 + j, 8 * k1, 8), part("BU", j), OP.subtract, to=soon)
        for j in range(2):
            later(tt, part("FA", j), B("CS", 32 * k0 + 15 + 16 * j, 32 * k1, 32), part("AB", j), OP.mult, to=soon)
        for j in range(2):
            later(tt, part("NB", j), part("FA", j), part("BU", j), OP.add, to=soon)
        later(end, to=soon)

    def right_place(k):
        ts(B("BU", 2 * k, 2 * k + 2), B("PQ", 8 * k + 6, 8 * k + 8), -float(E), OP.add)

    def place_diff(k):
        tt(B("AB", 2 * k, 2 * k + 2), B("PQ", 8 * k, 8 * k + 2), B("BU", 2 * k, 2 * k + 2), OP.subtract)

    def places(k):
        for j in range(2):
            ts(col("NU", 2 * k + j), col("CS", 32 * k + 15 + 16 * j), col("AB", 2 * k + j), OP.mult, col("BU", 2 * k + j), OP.add)
        list_out(k, "ex%d" % k)

    for t in range(R):
        last = t == R - 1

        def numbers():
            for b in range(4):
                act(B("VP", E * b, E * b + E), mm("QE", "SE", 128 * b, "QX", "SX", 0, E))

        if t == 0:
            table("s", 2)
        for k in range(8):
            score(k, C, E)
            if t == 0 and 1 <= k < 6:
                table("s", k + 2)
        if t:
            numbers()
        for k in range(8):
            if t == 0 and k == 3:
                quant("QE", "SE", 0, 512, "EB")
                numbers()
            o, c, n = E * k, 32 * k, 8 * k
            tt(B("GB"), B("SCP", o, o + 2 * E, ix=B("OF", n + 6, n + 8)), B("MINM"), OP.min)
            if 0 < k < 7:
                candidates(k)
                cp(B("PQ", n, n + 8), B("OF", n, n + 8))
            elif k == 7:
                cp(B("PQ", n + 6, n + 8), B("OF", n + 6, n + 8))
                cp(B("PQ", n, n + 2), B("OF", n, n + 2))
                spare()
            tt(B("GA"), B("SCP", o + E, o + 2 * E, ix=B("OF", n, n + 2)), B("GB"), OP.is_le)
            if 0 < k < 7:
                candidates_own(k)
            if 0 < k < 6:
                diff_ends(k)
            if k > 3:
                right_place(k)
            spare()
            scan(B("CS", c, c + 32), B("RM", 0, 32), B("GA"), OP.mult, OP.add)
            if 0 < k < 7:
                diff_candidates(k)
            if k > 3:
                place_diff(k)
            if k < 7:
                for x in range(4 if k < 6 else 0):
                    ts(col("OF", n + 8 + (4 + x if x < 2 else x)), col("CS", c + 15 + 16 * (x % 2)), col("D2", 4 * k + x), OP.mult, col("PQ", n + 4 + x), OP.add)
                spare()
                for x in (2, 3, 0, 1):
                    ts(col("OF", n + 8 + (4 + x if x > 1 else x)), col("CS", c + 15 + 16 * (x % 2)), col("D1", 4 * k + x), OP.mult,
                       col("SCN", 128 * k + 79 + 16 * x), OP.add)
                if k > 3:
                    places(k)
                elif k == 3:
                    lists_out(0, 4, "exa")
            else:
                while soon:
                    spare()
                places(k)
        while todo:
            todo.pop(0)()

        def flux(f, b):
            f(B("M", b, 1024, 4), B("VP", E * b, E * b + E, ix=B("OFN")))

        act(B("UNW"), B("IOTA", 0, E, ix=B("OFN")))
        for b in range(2):
            flux(cp, b)
            flux(act, b + 2)
        def equal(x):
            tt(B("EE", 256 * x, 256 * x + 256), B("NI", ix=B("REP", 16 * x, 16 * x + 16)), B("UNW"), OP.is_equal)

        cp(B("NI"), B("OFN"))
        ts(B("T1"), B("NI"), 0x1F0, OP.bitwise_and)
        equal(0)
        quant("QM", "SM", 0, C, "M")
        equal(1)
        tt(B("CEA"), B("NI"), B("T1"), OP.add)
        for x in range(2):
            scan(B("DS", 256 * x, 256 * x + 256), B("EE", 256 * x, 256 * x + 256), B("CDG", 256 * x, 256 * x + 256), OP.max, OP.mult)
        for x in range(2):
            ts(B("FLB", x, 16, 2), B("DS", 256 * x + 31, 256 * x + 256, 32), B("PF", 6, 7) if x else B("PF", 2, 3), OP.mult)
        tt(B("MXB"), B("CEA"), B("FLB"), OP.max)
        ts(B("OFS"), B("MXB"), B("PF", 3, 4), OP.add)
        cell = ("CELL%d" % (2 * t), "CELL%d" % (2 * t + 1))

        def scatter(w):
            cp(B(cell[w % 2], ix=B("OFS", 2 * w, 2 * w + 2)), B("POS", 32 * w, 32 * w + 32))

        for w in range(PRE):
            scatter(w)
        for b in range(4):
            act(B("TT", b, 1024, 4), mm("WQ", "WS", 128 * b, "QM", "SM", 0, C), scale=0.03125)
        quant("QT", "SQ", 0, C, "TT")
        for b in range(4):
            act(B("DW", PW * b + 1, PW * b + 257), mm("QE", "SE", 128 * b, "QT", "SQ", 0, C), scale=-1.0)
        for w in range(PRE, 8):
            scatter(w)
        for x in range(2):
            run("v", v.transpose, B("CT%d" % x), B(cell[x], 0, 768))
        for x in range(2):
            tt(B("CB" if x else "CA"), B("CT%d" % x, 0, 768, 32), B("CT%d" % x, 16, 768, 32), OP.max)
        tt(B("CM"), B("CA"), B("CB"), OP.max)
        cp(B("OFC"), B("CM"))

        def taken(b, w0, w1):
            return B("DW", PW * b, PW * b + 257, ix=B("OFC", w0, w1))

        for b in (0, 2, 1, 3):
            if b < 2:
                ts(B("UB", b, 512, 4), taken(b, 16, 24), -1.0, OP.mult)
            else:
                act(B("UB", b, 512, 4), taken(b, 16, 24), scale=-1.0)
        quant("QB", "SB", 0, 128, "UB")
        exchange(nxt, prv, ((B("LB", bit=dt.uint8), B("QB", bit=dt.uint8)), (B("LS"), B("SB"))), "bar", "sbar")
        for b in range(4):
            tt(B("X", 512 + b, 1024, 4), taken(b, 8, 16), B("VP", E * b + H, E * b + C), OP.add)
        quant("QX", "SX", H, C, "X")
        for b in range(4):
            tt(B("FU", H * b, H * b + H), taken(b, 0, 8), B("VP", E * b, E * b + H), OP.add)

        def result(a, b):
            act(B("YO", a, b), mm("QV", "SV", 0, "QX", "SX", a, b))
            sem = "outs" if a else "oute"
            dma("y", sem, T.oc[:, 4 * a:4 * b], B("QX", a, b, bit=dt.uint8))
            for k in range(4):
                dma("s" if a == 0 and k % 2 else "y", sem, T.osc[4 * k:4 * k + 4, a:b], B("SX", a, b, p=(32 * k, 32 * k + 4)))
            dma("s", sem, T.y[:, a:b], B("YO", a, b))

        if last:
            act(B("ONR"), B("UNW", ix=B("REV")))
            dma("y", "outs", T.on[:], (T.ONR[0:128:16, :], B("ONR")[1]))
            result(H, C)
        else:
            for k in range(EARLY):
                score(k, H, C)
        for b in range(4):
            tt(B("X", b, 512, 4), B("FU", H * b, H * b + H), mm("QE", "SE", 128 * b, "LB", "LS", 0, H), OP.subtract)
        quant("QX", "SX", 0, H, "X")
        if last:
            result(0, H)
        else:
            send_border()
            for k in range(8):
                score(k, 0, H if k < EARLY else C)
    for sem in SEMAPHORES:
        wait("g", sem, count[sem])
